import numpy as np, ml_dtypes
CORES = [35,38,43,46]
N = 4
import mx_ref
BF = ml_dtypes.bfloat16
def entries(a):
    return np.ascontiguousarray(a.T).reshape(-1)
def table(e):
    return np.ascontiguousarray(np.reshape(e, (-1, 16)).T).astype(np.int32)
def cols(t, e):
    v = np.concatenate([t.reshape(128, -1, 4), np.zeros((128, 1, 4), BF)], axis=1)
    return np.ascontiguousarray(v[:, e]).reshape(128, -1)
def cut(t, i, w=512):
    return t[:, w * i:w * i + w]
def f(rng, *shape):
    return mx_ref.flush((rng.standard_normal(shape, dtype=np.float32) * np.exp2(rng.integers(-2, 3, shape[:-1] + (1,)))).astype(BF))
def wide(rng, *shape, cols=0):
    v = rng.standard_normal(shape, dtype=np.float32) * np.exp2(rng.integers(-12, 13, shape)).astype(np.float32)
    if cols: v *= np.repeat(np.exp2(rng.integers(-cols, cols + 1, shape[:-2] + (1, shape[-1] // 4))) * (rng.random(shape[:-2] + (1, shape[-1] // 4)) > 0.0625), 4, axis=-1).astype(np.float32)
    return mx_ref.flush(v.astype(BF))
TB, T, CAPP, O = 512, 512, 64, 2
def lists(rng, case=""):
    o = []; odd = rng.permutation(N)
    for r in range(N):
        lo, hi = {"one": (1, 1), "full": (CAPP, CAPP), "runs": (1, CAPP // 2), "none": (1, CAPP)}.get(case, (0, CAPP))
        n = rng.integers(lo, hi + 1, N)
        if case == "none":
            if r == odd[0]: n[:] = 0; n[rng.integers(0, N)] = 1
            elif r == odd[1]: n[r] = 0
            elif r == odd[2]: n[np.arange(N) != r] = 0
            else: n[rng.permutation(N)[:rng.integers(1, N)]] = 0
        if n.sum() == 0: n[rng.integers(0, N)] = 1
        if case == "full": named = [np.append([0, TB - 1], 1 + rng.permutation(TB - 2)[:n[q] - 2]) for q in range(N)]
        else: named = [rng.permutation(TB)[:n[q]] for q in range(N)]
        pool = rng.permutation(np.concatenate([q * TB + named[q] for q in range(N)]))
        i = np.arange(len(pool))
        k = T - len(pool)
        i = np.concatenate([i, (rng.random(k) * rng.random(k) * len(pool)).astype(int)])
        i = np.sort(i) if case == "runs" else rng.permutation(i)
        o.append(table(pool[i]))
    return {"want": np.stack(o)}
def setup_inputs(rng):
    return {"x": f(rng, N, 128, 4 * TB), "w": f(rng, N, 128, 512 * O), **lists(rng)}
def setup_inputs_one(rng):
    return {**setup_inputs(rng), **lists(rng, "one")}
def setup_inputs_full(rng):
    return {**setup_inputs(rng), **lists(rng, "full")}
def setup_inputs_runs(rng):
    return {**setup_inputs(rng), **lists(rng, "runs")}
def setup_inputs_none(rng):
    return {**setup_inputs(rng), **lists(rng, "none")}
def setup_inputs_spread(rng):
    d = setup_inputs(rng); d["x"] = wide(rng, N, 128, 4 * TB, cols=8); return d
def check_inputs(d):
    b = []
    for r in range(N):
        e = entries(d["want"][r])
        if e.min() < 0 or e.max() >= N * TB or any(len(np.unique(e[e // TB == q])) > CAPP for q in range(N)): b.append("want")
    return b
def reference(x, w, want):
    every = np.concatenate([x[q] for q in range(N)], axis=1)
    y = np.zeros((N, 128, O * T), np.float32)
    for r in range(N):
        t = mx_ref.quantize(cols(every, entries(want[r])))
        for o in range(O):
            y[r][:, T * o:T * o + T] = mx_ref.matmul(mx_ref.quantize(np.ascontiguousarray(cut(w[r], o))), t)
    return {"y": y}

@@ -1,0 +1,365 @@
+from concourse.bass import DstId, RemoteDMATransfer
+from concourse.mybir import dt, AluOpType, ActivationFunctionType
+
+A = AluOpType
+F = ActivationFunctionType
+ROW = "float16"
+
+SCRATCH = {
+    "wl": ("sbuf", [128, 4], "int32"),
+    "wl16": ("sbuf", [128, 32], "int32"),
+    "pi": ("sbuf", [128, 1], "int32"),
+    "ci": ("sbuf", [128, 4], "float32"),
+    "i31": ("sbuf", [128, 1], "int32"),
+    "i15": ("sbuf", [128, 1], "int32"),
+    "i31f": ("sbuf", [128, 1], "float32"),
+    "i15f": ("sbuf", [128, 1], "float32"),
+    "lr": ("sbuf", [128, 32], "bfloat16"),
+    "d1": ("sbuf", [128, 320], "bfloat16"),
+    "s4b": ("sbuf", [128, 4], "float32"),
+    "lo": ("sbuf", [128, 2], "float32"),
+    "hi": ("sbuf", [128, 2], "float32"),
+    "ini": ("sbuf", [128, 2], "float32"),
+    "nb": ("sbuf", [128, 2], "float32"),
+    "twos": ("sbuf", [128, 32], "bfloat16"),
+    "qcol": ("sbuf", [128, 1], "float32"),
+    "base": ("sbuf", [128, 1], "float32"),
+    "base1": ("sbuf", [128, 1], "float32"),
+    "zeros": ("sbuf", [128, 512], "bfloat16"),
+    "ones": ("sbuf", [128, 64], "bfloat16"),
+    "wf": ("sbuf", [128, 4], "float32"),
+    "b1": ("sbuf", [128, 128], ROW),
+    "row": ("sbuf", [128, 128], ROW),
+    "ne": ("sbuf", [128, 320], "bfloat16"),
+    "dist": ("sbuf", [128, 320], "bfloat16"),
+    "soff": ("sbuf", [128, 4], "uint16"),
+    "win": ("sbuf", [128, 2112], "bfloat16"),
+    "wint": ("sbuf", [128, 2048], "bfloat16"),
+    "eo": ("sbuf", [128, 64], "float32"),
+    "e2": ("sbuf", [128, 64], "float32"),
+    "cn": ("sbuf", [128, 16], "float32"),
+    "b2": ("sbuf", [128, 512], "bfloat16"),
+    "row2": ("sbuf", [128, 544], "bfloat16"),
+    "pp": ("sbuf", [128, 256], "bfloat16"),
+    "po": ("sbuf", [128, 272], "bfloat16"),
+    "junk": ("sbuf", [128, 512], "bfloat16"),
+    "mk": ("sbuf", [128, 512], "bfloat16"),
+    "mks": ("sbuf", [128, 512], "bfloat16"),
+    "req": ("sbuf", [128, 4], "float32"),
+    "reqs": ("sbuf", [128, 12], "float32"),
+    "lown": ("sbuf", [128, 4], "uint16"),
+    "lrecv": ("sbuf", [128, 12], "uint16"),
+    "nn": ("sbuf", [128, 32], "int32"),
+    "qd": ("sbuf", [128, 32], "int32"),
+    "n5": ("sbuf", [128, 32], "float32"),
+    "ee": ("sbuf", [128, 32], "float32"),
+    "pm": ("sbuf", [128, 32], "float32"),
+    "off": ("sbuf", [128, 64], "uint16"),
+    "pb": ("sbuf", [128, 528], "bfloat16"),
+    "gs": ("sbuf", [128, 1024], "bfloat16"),
+    "tg": ("sbuf", [128, 1024], "bfloat16"),
+    "sa": ("sbuf", [128, 32], "float32"),
+    "sb": ("sbuf", [128, 32], "float32"),
+    "sc": ("sbuf", [128, 32], "float32"),
+    "slot": ("sbuf", [128, 32], "uint16"),
+    "xs": ("sbuf", [128, 2048], "bfloat16"),
+    "xp": ("sbuf", [128, 2064], "bfloat16"),
+    "tile": ("sbuf", [128, 1024], "bfloat16"),
+    "wt": ("sbuf", [128, 1024], "bfloat16"),
+    "wq": ("sbuf", [128, 256], "float8_e4m3fn_x4"),
+    "wsc": ("sbuf", [128, 256], "uint8"),
+    "qx": ("sbuf", [128, 448], "float8_e4m3fn_x4"),
+    "qs": ("sbuf", [128, 448], "uint8"),
+    "prod": ("psum", [128, 2048], "float32"),
+    "res": ("sbuf", [128, 512], "float32"),
+    "yt": ("sbuf", [128, 1024], "float32"),
+}
+SEMAPHORES = ["v", "s", "pe", "gi", "wl", "wl16", "x", "w", "y", "lists", "local", "arr_a", "arr_b"]
+
+
+def rank_program(g, core, T, topo):
+    me = T.rank_of(core)
+    if me is None:
+        return
+    cores = T.cores
+    S = T.sem
+
+    def near(q):
+        return topo.chip(cores[q]) == topo.chip(core)
+
+    def order(r):
+        o = [q for q in range(len(cores)) if q != r]
+        return sorted(o, key=lambda q: (topo.chip(cores[q]) != topo.chip(cores[r]), (q - r) % len(cores)))
+
+    mine = order(me)
+    away = [q for q in mine if not near(q)]
+    share = {}
+    far = []
+    for k, q in enumerate(away):
+        far = topo.engines(core, cores[q])
+        w = len(far) // len(away)
+        share[q] = far[k * w:(k + 1) * w]
+    for q in mine:
+        if q not in share:
+            share[q] = [e for e in topo.engines(core, cores[q]) if e not in far][::2]
+    masks = {q: sum(1 << e for e in share[q]) for q in mine}
+    n_near = sum(len(share[q]) for q in mine if near(q))
+    n_away = sum(len(share[q]) for q in away)
+
+    def dst(q):
+        rid, pid, _ = topo.addr(cores[q])
+        return [DstId(rid=rid, pnc=pid)]
+
+    cnt = {"v": 0, "s": 0}
+
+    def v(ins):
+        cnt["v"] += 1
+        ins.then_inc(S.v, 1)
+        return cnt["v"]
+
+    def s(ins):
+        cnt["s"] += 1
+        ins.then_inc(S.s, 1)
+        return cnt["s"]
+
+    V, SC = g.vector, g.scalar
+
+    g.sync.dma_start(T.wl[:], T.want[:]).then_inc(S.wl, 16)
+    g.sync.dma_start(T.xs[:], T.x[:]).then_inc(S.x, 16)
+    for a in range(8):
+        g.sync.dma_start(T.wl16[16 * a:16 * a + 16, :], T.want[:]).then_inc(S.wl16, 16)
+    g.sync.dma_start(T.wt[:], T.w[:]).then_inc(S.w, 16)
+
+    g.iota(T.pi[:], [[1, 1]], 0, 1).then_inc(S.gi, 1)
+    g.iota(T.ci[:], [[16, 4]], 0, 0, allow_small_or_imprecise_dtypes=True).then_inc(S.gi, 1)
+    g.iota(T.lr[:], [[1, 32]], 0, 0, allow_small_or_imprecise_dtypes=True).then_inc(S.gi, 1)
+    n_gi = 6
+    g.iota(T.pb[:, 512:528], [[0, 16]], 0, 0, allow_small_or_imprecise_dtypes=True).then_inc(S.gi, 1)
+    at = [64 * (0 if q == me else 1 + mine.index(q)) - 1 for q in range(4)]
+    both = ((T.qcol, [0, 1, 2, 3]), (T.base, at))
+    for t, val in both:
+        g.iota(t[:], [[0, 1]], val[3], 0, allow_small_or_imprecise_dtypes=True).then_inc(S.gi, 1)
+    for q in (2, 1, 0):
+        g.wait_ge(S.gi, n_gi)
+        for t, val in both:
+            g.affine_select(t[:], t[:], [[0, 1]], A.is_ge, float(val[q]), -32 * (q + 1), 1).then_inc(S.gi, 1)
+        n_gi += 2
+    i_z = v(V.memset(T.zeros[:], 0.0))
+    v(V.memset(T.d1[:], 4096.0))
+    V.wait_ge(S.gi, 3)
+    v(V.tensor_scalar(T.i31[:], T.pi[:], 31, None, A.bitwise_and))
+    i = v(V.tensor_scalar(T.i15[:], T.pi[:], 15, None, A.bitwise_and))
+    v(V.memset(T.ones[:], 1.0))
+    V.wait_ge(S.v, i)
+    v(V.tensor_copy(T.i31f[:], T.i31[:]))
+    i = v(V.tensor_copy(T.i15f[:], T.i15[:]))
+    V.wait_ge(S.v, i)
+    start = [0, 128, 224, 288]
+    for c in range(3):
+        v(V.tensor_scalar(T.d1[:, start[c]:start[c] + 32], T.lr[:], T.i31f[:, 0:1], -4096.0 * (96 - 32 * c), A.is_equal, A.mult))
+    v(V.tensor_scalar(T.d1[:, 288:319], T.lr[:, 0:31], T.i31f[:, 0:1], -4096.0, A.is_equal, A.mult))
+    v(V.tensor_scalar(T.d1[:, 319:320], T.i31f[:], 31.0, 4096.0, A.not_equal, A.mult))
+    i_s4 = v(V.tensor_scalar(T.s4b[:], T.ci[:], T.i15f[:, 0:1], 2048.0, A.add, A.add))
+    SC.wait_ge(S.v, i_z)
+    for k in range(4):
+        j_win = s(SC.activation(T.win[:, 512 * k:512 * k + 512], T.zeros[:], F.Copy))
+    s(SC.activation(T.row2[:, 0:32], T.zeros[:, 0:32], F.Copy))
+    s(SC.activation(T.twos[:], T.zeros[:, 0:32], F.Identity, bias=2.0))
+    SC.wait_ge(S.v, i_s4)
+    s(SC.activation(T.nb[:], T.s4b[:, 0:2], F.Identity, bias=4095.0, scale=-2.0))
+    s(SC.activation(T.lo[:], T.s4b[:, 2:4], F.Identity, bias=-4096.0, scale=2.0))
+    s(SC.activation(T.hi[:], T.s4b[:, 2:4], F.Identity, bias=-4094.0, scale=2.0))
+    j_con = s(SC.activation(T.ini[:], T.s4b[:, 2:4], F.Identity, bias=1048320.0, scale=-512.0))
+
+    V.wait_ge(S.wl, 16)
+    i = v(V.tensor_copy(T.wf[:], T.wl[:]))
+    V.wait_ge(S.v, i)
+    for c in range(4):
+        i = v(V.tensor_scalar(T.b1[:, 32 * c:32 * c + 32], T.zeros[:, 0:32], T.wf[:, c:c + 1], None, A.add))
+    V.wait_ge(S.v, i)
+    i = v(V.transpose(T.row[:], T.b1[:]))
+    V.wait_ge(S.v, i)
+    for c in range(4):
+        i = v(V.tensor_scalar(T.ne[:, start[c]:start[c] + 128 - 32 * c], T.row[:, 32 * c:128], T.wf[:, c:c + 1], None, A.not_equal))
+    V.wait_ge(S.v, i)
+    i = v(V.tensor_tensor_scan(T.dist[:], T.ne[:], T.d1[:], 0.0, A.mult, A.add))
+    V.wait_ge(S.v, i)
+    for c in range(4):
+        k = start[c] + 127 - 32 * c
+        i = v(V.tensor_scalar(T.soff[:, c:c + 1], T.dist[:, k:k + 1], T.wf[:, c:c + 1], T.s4b[:, c:c + 1], A.add, A.min))
+    V.wait_ge(S.v, i)
+    V.wait_ge(S.s, j_win)
+    i = v(V.tensor_copy(T.win[:, 0:2112].indirect(T.soff[:, 0:4]), T.ones[:]))
+
+    V.wait_ge(S.v, i)
+    i = v(V.transpose(T.wint[:], T.win[:, 0:2048]))
+    V.wait_ge(S.v, i)
+    i = v(V.tensor_tensor(T.eo[:], T.wint[:, 0:2048:32], T.wint[:, 16:2048:32], A.max))
+    V.wait_ge(S.v, i)
+    i = v(V.tensor_tensor(T.e2[0:64, :], T.eo[0:64, :], T.eo[64:128, :], A.max))
+    V.wait_ge(S.v, i)
+    for q in range(4):
+        c = slice(16 * q, 16 * q + 16)
+        i_cn = v(V.tensor_tensor(T.cn[32 * q:32 * q + 32, :], T.e2[0:32, c], T.e2[32:64, c], A.max))
+    SC.wait_ge(S.v, i_cn)
+    for b in range(7):
+        j = s(SC.activation(T.b2[:, 32 * b:32 * b + 32], T.zeros[:, 0:32], F.Identity, bias=T.cn[:, 8 + b:9 + b]))
+    V.wait_ge(S.v, i_cn)
+    V.wait_ge(S.s, j_con)
+    v(V.tensor_scalar(T.b2[:, 224:256], T.zeros[:, 0:32], T.cn[:, 15:16], None, A.add))
+    for b in range(8):
+        i = v(V.tensor_scalar(T.b2[:, 256 + 32 * b:288 + 32 * b], T.twos[:], T.cn[:, b:b + 1], T.cn[:, 8 + b:9 + b], A.mult, A.add))
+    V.wait_ge(S.v, i)
+    V.wait_ge(S.s, j)
+    i = v(V.transpose(T.row2[:, 32:544], T.b2[:]))
+    V.wait_ge(S.v, i)
+    i_p = v(V.tensor_tensor_scan(T.pp[:], T.row2[:, 288:544], T.row2[:, 31:287], 0.0, A.add, A.add))
+
+    SC.wait_ge(S.s, j_con)
+    SC.wait_ge(S.v, i_p)
+    for c in range(2):
+        j_cnt = s(SC.activation(T.junk[:, 256 * c:256 * c + 256], T.pp[:], F.Sign, bias=T.nb[:, c:c + 1], accum_out=T.req[:, c:c + 1]))
+    V.wait_ge(S.v, i_p)
+    m = [v(V.tensor_scalar(T.mk[:, 256 * c:256 * c + 256], T.pp[:], T.lo[:, c:c + 1], T.hi[:, c:c + 1], A.max, A.min)) for c in range(2)]
+    for c in range(2):
+        V.wait_ge(S.v, m[c])
+        k = slice(256 * c, 256 * c + 256)
+        i = v(V.tensor_tensor_scan(T.mks[:, k], T.mk[:, k], T.zeros[:, 0:256], T.ini[:, c:c + 1], A.add, A.add))
+    V.wait_ge(S.v, i)
+    i_req = v(V.tensor_copy(T.req[:, 2:4], T.mks[:, 255:512:256]))
+
+    g.wait_ge(S.s, j_cnt)
+    g.wait_ge(S.v, i_req)
+    tr = []
+    for q in mine:
+        at = 4 * order(q).index(me)
+        tr.append(RemoteDMATransfer(dst_ids=dst(q), dma_engine_mask=masks[q], remote_sem=S.lists,
+                                    src=T.req[:], dst=T.reqs[:, at:at + 4]))
+    g.remote_dma_fused(tr, local_sem=S.local)
+
+    V.wait_ge(S.x, 16)
+    SC.wait_ge(S.x, 16)
+    for t in range(2):
+        for o in range(2):
+            v(V.tensor_copy(T.xp[:, 512 * t + o:512 * t + 512:2], T.xs[:, 1024 * o + t:1024 * o + 1024:4]))
+    for t in range(2, 4):
+        for o in range(2):
+            j_xp = s(SC.activation(T.xp[:, 512 * t + o:512 * t + 512:2], T.xs[:, 1024 * o + t:1024 * o + 1024:4], F.Copy))
+    v(V.memset(T.xp[:, 2048:2064], 0.0))
+    i = v(V.memset(T.po[:, 0:16], 0.0))
+    i_po = v(V.tensor_tensor_scan(T.po[:, 16:272], T.row2[:, 288:544], T.row2[:, 32:288], 0.0, A.add, A.add))
+    V.wait_ge(S.v, i_req)
+    V.wait_ge(S.s, j_cnt)
+    for a in range(4):
+        i_own = v(V.tensor_scalar(T.lown[32 * a:32 * a + 32, :], T.req[32 * me:32 * me + 32, :], -1.0, 256.0, A.mult, A.add))
+    V.wait_ge(S.v, i_own)
+    V.wait_ge(S.s, j_xp - 2)
+    for t in range(2):
+        v(V.tensor_copy(T.tile[:, 768 + t:1024:4], T.xp[:, 512 * t:512 * t + 528].indirect(T.lown[:, 0:4])))
+    SC.wait_ge(S.s, j_xp)
+    SC.wait_ge(S.v, i_own)
+    for t in range(2, 4):
+        s(SC.activation(T.tile[:, 768 + t:1024:4], T.xp[:, 512 * t:512 * t + 528].indirect(T.lown[:, 0:4]), F.Copy))
+    V.wait_ge(S.w, 16)
+    v(V.quantize_mx(T.wq[:, 0:256], T.wsc[:, 0:256], T.wt[:]))
+    V.wait_ge(S.gi, n_gi)
+    V.wait_ge(S.wl16, 128)
+    v(V.tensor_scalar(T.nn[:], T.wl16[:], 511, None, A.bitwise_and))
+    i = v(V.tensor_scalar(T.qd[:], T.wl16[:], 9, None, A.logical_shift_right))
+    V.wait_ge(S.v, i)
+    v(V.tensor_scalar(T.n5[:], T.nn[:], -512.0, None, A.add))
+    i = v(V.tensor_scalar(T.ee[:], T.qd[:], T.qcol[:, 0:1], None, A.is_equal))
+    V.wait_ge(S.v, i)
+    i = v(V.tensor_tensor(T.pm[:], T.n5[:], T.ee[:], A.mult))
+    V.wait_ge(S.v, i)
+    v(V.tensor_scalar(T.off[:, 0:64:2], T.pm[:], 512.0, None, A.add))
+    i_off = v(V.tensor_scalar(T.off[:, 1:64:2], T.pm[:], 512.0, None, A.add))
+    SC.wait_ge(S.gi, n_gi)
+    j = s(SC.activation(T.base1[:], T.base[:], F.Identity, bias=1.0))
+    SC.wait_ge(S.v, i_po)
+    s(SC.activation(T.pb[:, 256:512], T.po[:, 16:272], F.Identity, bias=T.base[:, 0:1], scale=0.5))
+    SC.wait_ge(S.s, j)
+    j_pb = s(SC.activation(T.pb[:, 0:256], T.po[:, 15:271], F.Identity, bias=T.base1[:, 0:1], scale=0.5))
+
+    V.wait_ge(S.lists, n_near + n_away)
+    for a in range(4):
+        i_l = v(V.tensor_scalar(T.lrecv[32 * a:32 * a + 32, :], T.reqs[32 * me:32 * me + 32, :], -1.0, 256.0, A.mult, A.add))
+    SC.wait_ge(S.v, i_l)
+    V.wait_ge(S.v, i_l)
+    for t in range(2):
+        i = v(V.tensor_copy(T.tile[:, t:768:4], T.xp[:, 512 * t:512 * t + 528].indirect(T.lrecv[:, 0:12])))
+    for t in range(2, 4):
+        j = s(SC.activation(T.tile[:, t:768:4], T.xp[:, 512 * t:512 * t + 528].indirect(T.lrecv[:, 0:12]), F.Copy))
+    V.wait_ge(S.v, i)
+    V.wait_ge(S.s, j)
+    i_q = v(V.quantize_mx(T.qx[:, 0:256], T.qs[:, 0:256], T.tile[:]))
+
+    g.wait_ge(S.v, i_q)
+    for codes in (True, False):
+        tr = []
+        for k, q in enumerate(mine):
+            at = 256 + 64 * order(q).index(me)
+            if codes:
+                a, b = T.qx[:, 64 * k:64 * k + 64].bitcast(dt.uint8), T.qx[:, at:at + 64].bitcast(dt.uint8)
+            else:
+                a, b = T.qs[:, 64 * k:64 * k + 64], T.qs[:, at:at + 64]
+            tr.append(RemoteDMATransfer(dst_ids=dst(q), dma_engine_mask=masks[q], remote_sem=S.arr_a if near(q) else S.arr_b, src=a, dst=b))
+        g.remote_dma_fused(tr, local_sem=S.local)
+    g.wait_ge(S.local, 3 * (n_near + n_away))
+
+    V.wait_ge(S.s, j_pb)
+    V.wait_ge(S.v, i_off)
+    i = v(V.tensor_copy(T.gs[:, 0:512], T.pb[:, 0:528].indirect(T.off[:, 0:32])))
+    SC.wait_ge(S.v, i_off)
+    SC.wait_ge(S.s, j_pb)
+    j = s(SC.activation(T.gs[:, 512:1024], T.pb[:, 0:528].indirect(T.off[:, 32:64]), F.Copy))
+    V.wait_ge(S.v, i)
+    V.wait_ge(S.s, j)
+    i = v(V.transpose(T.tg[:], T.gs[:]))
+    V.wait_ge(S.v, i)
+    v(V.tensor_tensor(T.sa[0:32, :], T.tg[0:32, 0:1024:32], T.tg[32:64, 0:1024:32], A.add))
+    i = v(V.tensor_tensor(T.sb[0:32, :], T.tg[64:96, 0:1024:32], T.tg[96:128, 0:1024:32], A.add))
+    V.wait_ge(S.v, i)
+    i = v(V.tensor_tensor(T.sc[0:32, :], T.sa[0:32, :], T.sb[0:32, :], A.add))
+    V.wait_ge(S.v, i)
+    for a in range(4):
+        v(V.tensor_copy(T.slot[32 * a:32 * a + 32, :], T.sc[0:32, :]))
+
+    g.tensor.wait_ge(S.v, i_q)
+    pe = {}
+    for h in range(2):
+        if h == 0:
+            g.tensor.wait_ge(S.arr_a, 2 * n_near)
+        else:
+            g.tensor.wait_ge(S.arr_b, 2 * n_away)
+        c = slice(192 + 128 * h, 320 + 128 * h)
+        for o in range(2):
+            k = 2 * o + h
+            g.tensor.matmul_mx(T.prod[:, 512 * k:512 * k + 128], T.wq[:, 128 * o:128 * o + 128], T.wsc[:, 128 * o:128 * o + 128],
+                               T.qx[:, c], T.qs[:, c], True, True).then_inc(S.pe, 1)
+            pe[(o, h)] = len(pe) + 1
+    SC.wait_ge(S.pe, pe[(1, 0)])
+    s(SC.activation(T.res[:, 256:384], T.prod[:, 1024:1152], F.Copy))
+    for h in range(2):
+        V.wait_ge(S.pe, pe[(0, h)])
+        i = v(V.tensor_copy(T.res[:, 128 * h:128 * h + 128], T.prod[:, 512 * h:512 * h + 128]))
+
+    for e in range(4):
+        o, k = e // 2, 16 * (e % 2)
+        c = 256 * e
+        r = slice(256 * o, 256 * o + 256)
+        if e == 0:
+            V.wait_ge(S.v, i)
+            SC.wait_ge(S.v, i)
+        if e == 2:
+            V.wait_ge(S.s, j)
+            SC.wait_ge(S.s, j)
+        a = v(V.tensor_copy(T.yt[:, c:c + 128], T.res[:, r].indirect(T.slot[:, k:k + 8])))
+        b = s(SC.activation(T.yt[:, c + 128:c + 256], T.res[:, r].indirect(T.slot[:, k + 8:k + 16]), F.Copy))
+        if e == 0:
+            SC.wait_ge(S.pe, pe[(1, 1)])
+            j = s(SC.activation(T.res[:, 384:512], T.prod[:, 1536:1664], F.Copy))
+        g.sync.wait_ge(S.v, a)
+        g.sync.wait_ge(S.s, b)
+        g.sync.dma_start(T.y[:, c:c + 256], T.yt[:, c:c + 256]).then_inc(S.y, 16)
+    g.sync.wait_ge(S.y, 64)

@@ -7,36 +7,32 @@ ROW = "float16"
 
 SCRATCH = {
     "wl": ("sbuf", [128, 4], "int32"),
-    "wl16": ("sbuf", [128, 32], "int32"),
-    "pi": ("sbuf", [128, 1], "int32"),
+    "wl16": ("sbuf", [128, 16], "int32"),
+    "ramp": ("sbuf", [128, 193], "bfloat16"),
+    "lane": ("sbuf", [128, 32], "bfloat16"),
+    "dump": ("sbuf", [128, 4], "float32"),
     "ci": ("sbuf", [128, 4], "float32"),
-    "i31": ("sbuf", [128, 1], "int32"),
-    "i15": ("sbuf", [128, 1], "int32"),
-    "i31f": ("sbuf", [128, 1], "float32"),
-    "i15f": ("sbuf", [128, 1], "float32"),
-    "lr": ("sbuf", [128, 32], "bfloat16"),
-    "d1": ("sbuf", [128, 320], "bfloat16"),
-    "s4b": ("sbuf", [128, 4], "float32"),
+    "la": ("sbuf", [128, 1], "float32"),
+    "lb": ("sbuf", [128, 1], "float32"),
+    "lc": ("sbuf", [128, 1], "float32"),
+    "d1": ("sbuf", [128, 420], "bfloat16"),
+    "nb": ("sbuf", [128, 4], "float32"),
     "lo": ("sbuf", [128, 2], "float32"),
     "hi": ("sbuf", [128, 2], "float32"),
     "ini": ("sbuf", [128, 2], "float32"),
-    "nb": ("sbuf", [128, 2], "float32"),
-    "twos": ("sbuf", [128, 32], "bfloat16"),
-    "qcol": ("sbuf", [128, 1], "float32"),
-    "base": ("sbuf", [128, 1], "float32"),
-    "base1": ("sbuf", [128, 1], "float32"),
-    "zeros": ("sbuf", [128, 512], "bfloat16"),
+    "pat": ("sbuf", [128, 64], "bfloat16"),
+    "qb": ("sbuf", [128, 4], "float32"),
     "ones": ("sbuf", [128, 64], "bfloat16"),
     "wf": ("sbuf", [128, 4], "float32"),
     "b1": ("sbuf", [128, 128], ROW),
     "row": ("sbuf", [128, 128], ROW),
-    "ne": ("sbuf", [128, 320], "bfloat16"),
-    "dist": ("sbuf", [128, 320], "bfloat16"),
-    "soff": ("sbuf", [128, 4], "uint16"),
-    "win": ("sbuf", [128, 2112], "bfloat16"),
-    "wint": ("sbuf", [128, 2048], "bfloat16"),
-    "eo": ("sbuf", [128, 64], "float32"),
-    "e2": ("sbuf", [128, 64], "float32"),
+    "eq": ("sbuf", [128, 420], ROW),
+    "dist": ("sbuf", [128, 420], ROW),
+    "half": ("sbuf", [128, 1], "float32"),
+    "soff": ("sbuf", [128, 8], "uint16"),
+    "win": ("sbuf", [128, 4096], "bfloat16"),
+    "wint": ("sbuf", [128, 1024], "bfloat16"),
+    "e2": ("sbuf", [128, 32], "bfloat16"),
     "cn": ("sbuf", [128, 16], "float32"),
     "b2": ("sbuf", [128, 512], "bfloat16"),
     "row2": ("sbuf", [128, 544], "bfloat16"),
@@ -44,22 +40,16 @@ SCRATCH = {
     "po": ("sbuf", [128, 272], "bfloat16"),
     "junk": ("sbuf", [128, 512], "bfloat16"),
     "mk": ("sbuf", [128, 512], "bfloat16"),
-    "mks": ("sbuf", [128, 512], "bfloat16"),
-    "req": ("sbuf", [128, 4], "float32"),
+    "req": ("sbuf", [128, 260], "float32"),
     "reqs": ("sbuf", [128, 12], "float32"),
     "lown": ("sbuf", [128, 4], "uint16"),
     "lrecv": ("sbuf", [128, 12], "uint16"),
-    "nn": ("sbuf", [128, 32], "int32"),
-    "qd": ("sbuf", [128, 32], "int32"),
-    "n5": ("sbuf", [128, 32], "float32"),
-    "ee": ("sbuf", [128, 32], "float32"),
-    "pm": ("sbuf", [128, 32], "float32"),
-    "off": ("sbuf", [128, 64], "uint16"),
-    "pb": ("sbuf", [128, 528], "bfloat16"),
-    "gs": ("sbuf", [128, 1024], "bfloat16"),
-    "tg": ("sbuf", [128, 1024], "bfloat16"),
+    "nn": ("sbuf", [128, 16], "float32"),
+    "off": ("sbuf", [128, 32], "uint16"),
+    "pb": ("sbuf", [128, 514], "bfloat16"),
+    "gs": ("sbuf", [128, 512], "bfloat16"),
+    "tg": ("sbuf", [128, 512], "bfloat16"),
     "sa": ("sbuf", [128, 32], "float32"),
-    "sb": ("sbuf", [128, 32], "float32"),
     "sc": ("sbuf", [128, 32], "float32"),
     "slot": ("sbuf", [128, 32], "uint16"),
     "xs": ("sbuf", [128, 2048], "bfloat16"),
@@ -110,7 +100,7 @@ def rank_program(g, core, T, topo):
         rid, pid, _ = topo.addr(cores[q])
         return [DstId(rid=rid, pnc=pid)]
 
-    cnt = {"v": 0, "s": 0}
+    cnt = {"v": 0, "s": 0, "gi": 0}
 
     def v(ins):
         cnt["v"] += 1
@@ -122,111 +112,118 @@ def rank_program(g, core, T, topo):
         ins.then_inc(S.s, 1)
         return cnt["s"]
 
+    def iota(out, pattern, base, step=0):
+        cnt["gi"] += 1
+        g.iota(out, pattern, base, step, allow_small_or_imprecise_dtypes=True).then_inc(S.gi, 1)
+        return cnt["gi"]
+
     V, SC = g.vector, g.scalar
 
     g.sync.dma_start(T.wl[:], T.want[:]).then_inc(S.wl, 16)
     g.sync.dma_start(T.xs[:], T.x[:]).then_inc(S.x, 16)
     for a in range(8):
-        g.sync.dma_start(T.wl16[16 * a:16 * a + 16, :], T.want[:]).then_inc(S.wl16, 16)
+        h = 16 * (a % 2)
+        g.sync.dma_start(T.wl16[16 * a:16 * a + 16, :], T.want[:, h:h + 16]).then_inc(S.wl16, 16)
     g.sync.dma_start(T.wt[:], T.w[:]).then_inc(S.w, 16)
 
-    g.iota(T.pi[:], [[1, 1]], 0, 1).then_inc(S.gi, 1)
-    g.iota(T.ci[:], [[16, 4]], 0, 0, allow_small_or_imprecise_dtypes=True).then_inc(S.gi, 1)
-    g.iota(T.lr[:], [[1, 32]], 0, 0, allow_small_or_imprecise_dtypes=True).then_inc(S.gi, 1)
-    n_gi = 6
-    g.iota(T.pb[:, 512:528], [[0, 16]], 0, 0, allow_small_or_imprecise_dtypes=True).then_inc(S.gi, 1)
-    at = [64 * (0 if q == me else 1 + mine.index(q)) - 1 for q in range(4)]
-    both = ((T.qcol, [0, 1, 2, 3]), (T.base, at))
-    for t, val in both:
-        g.iota(t[:], [[0, 1]], val[3], 0, allow_small_or_imprecise_dtypes=True).then_inc(S.gi, 1)
-    for q in (2, 1, 0):
-        g.wait_ge(S.gi, n_gi)
-        for t, val in both:
-            g.affine_select(t[:], t[:], [[0, 1]], A.is_ge, float(val[q]), -32 * (q + 1), 1).then_inc(S.gi, 1)
-        n_gi += 2
-    i_z = v(V.memset(T.zeros[:], 0.0))
-    v(V.memset(T.d1[:], 4096.0))
-    V.wait_ge(S.gi, 3)
-    v(V.tensor_scalar(T.i31[:], T.pi[:], 31, None, A.bitwise_and))
-    i = v(V.tensor_scalar(T.i15[:], T.pi[:], 15, None, A.bitwise_and))
+    k_ramp = iota(T.ramp[:], [[1, 193]], -64)
+    k_dump = iota(T.dump[:], [[2, 4]], 2048, 8)
+    k_ci = iota(T.ci[:], [[-32, 4]], 0)
+    k_pat = iota(T.pat[:], [[0, 32], [-2, 2]], 2)
+    k_pad = iota(T.row2[:, 30:32], [[0, 2]], 0)
+    iota(T.po[:, 14:16], [[0, 2]], 0)
+    iota(T.pb[:, 0:514:513], [[0, 2]], 0)
+    for q in range(4):
+        at = 64 * (0 if q == me else 1 + mine.index(q)) - 1
+        g.wait_ge(S.gi, cnt["gi"])
+        k_all = iota(T.qb[32 * q:32 * q + 32, :], [[1 - 512 * q - at, 2], [1, 2]], at)
+    i_z = v(V.memset(T.win[:, 1024:1280], 0.0))
     v(V.memset(T.ones[:], 1.0))
-    V.wait_ge(S.v, i)
-    v(V.tensor_copy(T.i31f[:], T.i31[:]))
-    i = v(V.tensor_copy(T.i15f[:], T.i15[:]))
-    V.wait_ge(S.v, i)
-    start = [0, 128, 224, 288]
-    for c in range(3):
-        v(V.tensor_scalar(T.d1[:, start[c]:start[c] + 32], T.lr[:], T.i31f[:, 0:1], -4096.0 * (96 - 32 * c), A.is_equal, A.mult))
-    v(V.tensor_scalar(T.d1[:, 288:319], T.lr[:, 0:31], T.i31f[:, 0:1], -4096.0, A.is_equal, A.mult))
-    v(V.tensor_scalar(T.d1[:, 319:320], T.i31f[:], 31.0, 4096.0, A.not_equal, A.mult))
-    i_s4 = v(V.tensor_scalar(T.s4b[:], T.ci[:], T.i15f[:, 0:1], 2048.0, A.add, A.add))
+    v(V.memset(T.half[0:64, :], 1024.0))
+    v(V.memset(T.half[64:128, :], 0.0))
+    V.wait_ge(S.gi, k_ramp)
+    i_lane = v(V.transpose(T.lane[:], T.ramp[:, 64:96]))
+    V.wait_ge(S.v, i_lane)
+    start, first = [0, 129, 226, 323], [0, 32, 32, 32]
+    for c in range(4):
+        n, a = 129 - first[c], 64 + first[c] - 32 * c
+        v(V.tensor_scalar(T.d1[:, start[c]:start[c] + n], T.ramp[:, a:a + n], T.lane[:, 0:1], 4096.0, A.not_equal, A.mult))
     SC.wait_ge(S.v, i_z)
-    for k in range(4):
-        j_win = s(SC.activation(T.win[:, 512 * k:512 * k + 512], T.zeros[:], F.Copy))
-    s(SC.activation(T.row2[:, 0:32], T.zeros[:, 0:32], F.Copy))
-    s(SC.activation(T.twos[:], T.zeros[:, 0:32], F.Identity, bias=2.0))
-    SC.wait_ge(S.v, i_s4)
-    s(SC.activation(T.nb[:], T.s4b[:, 0:2], F.Identity, bias=4095.0, scale=-2.0))
-    s(SC.activation(T.lo[:], T.s4b[:, 2:4], F.Identity, bias=-4096.0, scale=2.0))
-    s(SC.activation(T.hi[:], T.s4b[:, 2:4], F.Identity, bias=-4094.0, scale=2.0))
-    j_con = s(SC.activation(T.ini[:], T.s4b[:, 2:4], F.Identity, bias=1048320.0, scale=-512.0))
+    for k in range(1, 4):
+        j_win = s(SC.activation(T.win[:, 1024 + 256 * k:1280 + 256 * k], T.win[:, 1024:1280], F.Copy))
+    SC.wait_ge(S.v, i_lane)
+    s(SC.activation(T.la[:], T.lane[:, 0:1], F.Sign, bias=-15.5))
+    j = s(SC.activation(T.lb[:], T.lane[:, 0:1], F.Identity, bias=15.0, scale=-2.0))
+    SC.wait_ge(S.s, j)
+    j = s(SC.activation(T.lc[:], T.la[:], F.Identity, bias=T.lb[:, 0:1], scale=16.0))
+    SC.wait_ge(S.s, j)
+    SC.wait_ge(S.gi, k_pat)
+    j = s(SC.activation(T.nb[:], T.ci[:], F.Identity, bias=T.lc[:, 0:1]))
+    SC.wait_ge(S.s, j)
+    s(SC.activation(T.lo[:], T.nb[:, 0:2], F.Identity, bias=-1.0, scale=-1.0))
+    s(SC.activation(T.hi[:], T.nb[:, 0:2], F.Identity, bias=1.0, scale=-1.0))
+    j_con = s(SC.activation(T.ini[:], T.nb[:, 0:2], F.Identity, bias=16.0, scale=256.0))
 
     V.wait_ge(S.wl, 16)
     i = v(V.tensor_copy(T.wf[:], T.wl[:]))
     V.wait_ge(S.v, i)
     for c in range(4):
-        i = v(V.tensor_scalar(T.b1[:, 32 * c:32 * c + 32], T.zeros[:, 0:32], T.wf[:, c:c + 1], None, A.add))
+        i = v(V.tensor_scalar(T.b1[:, 32 * c:32 * c + 32], T.win[:, 1024:1056], T.wf[:, c:c + 1], None, A.add))
+    v(V.tensor_copy(T.eq[:, 128:420:97], T.wf[:]))
     V.wait_ge(S.v, i)
     i = v(V.transpose(T.row[:], T.b1[:]))
     V.wait_ge(S.v, i)
+    V.wait_ge(S.gi, k_dump)
     for c in range(4):
-        i = v(V.tensor_scalar(T.ne[:, start[c]:start[c] + 128 - 32 * c], T.row[:, 32 * c:128], T.wf[:, c:c + 1], None, A.not_equal))
+        i = v(V.tensor_scalar(T.eq[:, start[c]:start[c] + 128 - first[c]], T.row[:, first[c]:128], T.wf[:, c:c + 1], T.dump[:, c:c + 1],
+                              A.is_equal, A.mult))
     V.wait_ge(S.v, i)
-    i = v(V.tensor_tensor_scan(T.dist[:], T.ne[:], T.d1[:], 0.0, A.mult, A.add))
+    i = v(V.tensor_tensor_scan(T.dist[:], T.eq[:], T.d1[:], 0.0, A.max, A.min))
     V.wait_ge(S.v, i)
-    for c in range(4):
-        k = start[c] + 127 - 32 * c
-        i = v(V.tensor_scalar(T.soff[:, c:c + 1], T.dist[:, k:k + 1], T.wf[:, c:c + 1], T.s4b[:, c:c + 1], A.add, A.min))
+    ends = slice(128, 420, 97)
+    i = v(V.tensor_scalar(T.soff[:, 0:4], T.dist[:, ends], T.half[:, 0:1], None, A.add))
+    v(V.tensor_scalar(T.soff[0:64, 4:8], T.dist[64:128, ends], 1024.0, None, A.add))
     V.wait_ge(S.v, i)
     V.wait_ge(S.s, j_win)
-    i = v(V.tensor_copy(T.win[:, 0:2112].indirect(T.soff[:, 0:4]), T.ones[:]))
+    v(V.tensor_copy(T.win[:, 0:4096].indirect(T.soff[:, 0:4]), T.ones[:]))
+    i = v(V.tensor_scalar(T.soff[64:128, 4:8], T.dist[0:64, ends], 0.0, None, A.add))
+    V.wait_ge(S.v, i)
+    i = v(V.tensor_copy(T.win[:, 0:4096].indirect(T.soff[:, 4:8]), T.ones[:]))
 
     V.wait_ge(S.v, i)
-    i = v(V.transpose(T.wint[:], T.win[:, 0:2048]))
-    V.wait_ge(S.v, i)
-    i = v(V.tensor_tensor(T.eo[:], T.wint[:, 0:2048:32], T.wint[:, 16:2048:32], A.max))
-    V.wait_ge(S.v, i)
-    i = v(V.tensor_tensor(T.e2[0:64, :], T.eo[0:64, :], T.eo[64:128, :], A.max))
+    i = v(V.transpose(T.wint[:], T.win[:, 1024:2048]))
     V.wait_ge(S.v, i)
     for q in range(4):
-        c = slice(16 * q, 16 * q + 16)
-        i_cn = v(V.tensor_tensor(T.cn[32 * q:32 * q + 32, :], T.e2[0:32, c], T.e2[32:64, c], A.max))
-    SC.wait_ge(S.v, i_cn)
-    for b in range(7):
-        j = s(SC.activation(T.b2[:, 32 * b:32 * b + 32], T.zeros[:, 0:32], F.Identity, bias=T.cn[:, 8 + b:9 + b]))
-    V.wait_ge(S.v, i_cn)
-    V.wait_ge(S.s, j_con)
-    v(V.tensor_scalar(T.b2[:, 224:256], T.zeros[:, 0:32], T.cn[:, 15:16], None, A.add))
-    for b in range(8):
-        i = v(V.tensor_scalar(T.b2[:, 256 + 32 * b:288 + 32 * b], T.twos[:], T.cn[:, b:b + 1], T.cn[:, 8 + b:9 + b], A.mult, A.add))
+        a, c = 64 * (q // 2), slice(512 * (q % 2), 512 * (q % 2) + 512, 16)
+        i = v(V.tensor_tensor(T.e2[32 * q:32 * q + 32, :], T.wint[a:a + 32, c], T.wint[a + 32:a + 64, c], A.max))
     V.wait_ge(S.v, i)
-    V.wait_ge(S.s, j)
-    i = v(V.transpose(T.row2[:, 32:544], T.b2[:]))
+    i_cn = v(V.tensor_tensor(T.cn[:], T.e2[:, 0:32:2], T.e2[:, 1:32:2], A.max))
+    SC.wait_ge(S.v, i_cn)
+    for b in range(4, 8):
+        j = s(SC.activation(T.b2[:, 64 * b:64 * b + 64], T.pat[:], F.Identity, bias=T.cn[:, 8 + b:9 + b], scale=T.cn[:, b:b + 1]))
+    V.wait_ge(S.v, i_cn)
+    V.wait_ge(S.gi, k_pad)
+    for b in range(4):
+        i = v(V.tensor_scalar(T.b2[:, 64 * b:64 * b + 64], T.pat[:], T.cn[:, b:b + 1], T.cn[:, 8 + b:9 + b], A.mult, A.add))
+    V.wait_ge(S.v, i)
+    for h in range(2):
+        if h == 1:
+            V.wait_ge(S.s, j)
+        v(V.transpose(T.row2[:, 288 + 128 * h:416 + 128 * h], T.b2[:, 256 * h:256 * h + 256:2]))
+        i = v(V.transpose(T.row2[:, 32 + 128 * h:160 + 128 * h], T.b2[:, 256 * h + 1:256 * h + 256:2]))
     V.wait_ge(S.v, i)
     i_p = v(V.tensor_tensor_scan(T.pp[:], T.row2[:, 288:544], T.row2[:, 31:287], 0.0, A.add, A.add))
 
-    SC.wait_ge(S.s, j_con)
     SC.wait_ge(S.v, i_p)
-    for c in range(2):
-        j_cnt = s(SC.activation(T.junk[:, 256 * c:256 * c + 256], T.pp[:], F.Sign, bias=T.nb[:, c:c + 1], accum_out=T.req[:, c:c + 1]))
+    for c in range(2, 4):
+        j_cnt = s(SC.activation(T.junk[:, 256 * c - 512:256 * c - 272], T.pp[:, 16:256], F.Sign, bias=T.nb[:, c:c + 1],
+                                accum_out=T.req[:, 256 + c:257 + c]))
     V.wait_ge(S.v, i_p)
     m = [v(V.tensor_scalar(T.mk[:, 256 * c:256 * c + 256], T.pp[:], T.lo[:, c:c + 1], T.hi[:, c:c + 1], A.max, A.min)) for c in range(2)]
     for c in range(2):
         V.wait_ge(S.v, m[c])
-        k = slice(256 * c, 256 * c + 256)
-        i = v(V.tensor_tensor_scan(T.mks[:, k], T.mk[:, k], T.zeros[:, 0:256], T.ini[:, c:c + 1], A.add, A.add))
-    V.wait_ge(S.v, i)
-    i_req = v(V.tensor_copy(T.req[:, 2:4], T.mks[:, 255:512:256]))
+        k = 256 * c
+        i_req = v(V.tensor_tensor_scan(T.req[:, 2 + c:258:2], T.mk[:, k:k + 128], T.mk[:, k + 128:k + 256], T.ini[:, c:c + 1], A.add, A.add))
 
     g.wait_ge(S.s, j_cnt)
     g.wait_ge(S.v, i_req)
@@ -234,7 +231,7 @@ def rank_program(g, core, T, topo):
     for q in mine:
         at = 4 * order(q).index(me)
         tr.append(RemoteDMATransfer(dst_ids=dst(q), dma_engine_mask=masks[q], remote_sem=S.lists,
-                                    src=T.req[:], dst=T.reqs[:, at:at + 4]))
+                                    src=T.req[:, 256:260], dst=T.reqs[:, at:at + 4]))
     g.remote_dma_fused(tr, local_sem=S.local)
 
     V.wait_ge(S.x, 16)
@@ -246,44 +243,23 @@ def rank_program(g, core, T, topo):
         for o in range(2):
             j_xp = s(SC.activation(T.xp[:, 512 * t + o:512 * t + 512:2], T.xs[:, 1024 * o + t:1024 * o + 1024:4], F.Copy))
     v(V.memset(T.xp[:, 2048:2064], 0.0))
-    i = v(V.memset(T.po[:, 0:16], 0.0))
     i_po = v(V.tensor_tensor_scan(T.po[:, 16:272], T.row2[:, 288:544], T.row2[:, 32:288], 0.0, A.add, A.add))
     V.wait_ge(S.v, i_req)
     V.wait_ge(S.s, j_cnt)
     for a in range(4):
-        i_own = v(V.tensor_scalar(T.lown[32 * a:32 * a + 32, :], T.req[32 * me:32 * me + 32, :], -1.0, 256.0, A.mult, A.add))
+        i_own = v(V.tensor_scalar(T.lown[32 * a:32 * a + 32, :], T.req[32 * me:32 * me + 32, 256:260], -1.0, 272.0, A.mult, A.add))
     V.wait_ge(S.v, i_own)
     V.wait_ge(S.s, j_xp - 2)
     for t in range(2):
-        v(V.tensor_copy(T.tile[:, 768 + t:1024:4], T.xp[:, 512 * t:512 * t + 528].indirect(T.lown[:, 0:4])))
+        i = v(V.tensor_copy(T.tile[:, 768 + t:1024:4], T.xp[:, 512 * t:512 * t + 528].indirect(T.lown[:, 0:4])))
     SC.wait_ge(S.s, j_xp)
     SC.wait_ge(S.v, i_own)
     for t in range(2, 4):
-        s(SC.activation(T.tile[:, 768 + t:1024:4], T.xp[:, 512 * t:512 * t + 528].indirect(T.lown[:, 0:4]), F.Copy))
-    V.wait_ge(S.w, 16)
-    v(V.quantize_mx(T.wq[:, 0:256], T.wsc[:, 0:256], T.wt[:]))
-    V.wait_ge(S.gi, n_gi)
-    V.wait_ge(S.wl16, 128)
-    v(V.tensor_scalar(T.nn[:], T.wl16[:], 511, None, A.bitwise_and))
-    i = v(V.tensor_scalar(T.qd[:], T.wl16[:], 9, None, A.logical_shift_right))
-    V.wait_ge(S.v, i)
-    v(V.tensor_scalar(T.n5[:], T.nn[:], -512.0, None, A.add))
-    i = v(V.tensor_scalar(T.ee[:], T.qd[:], T.qcol[:, 0:1], None, A.is_equal))
-    V.wait_ge(S.v, i)
-    i = v(V.tensor_tensor(T.pm[:], T.n5[:], T.ee[:], A.mult))
-    V.wait_ge(S.v, i)
-    v(V.tensor_scalar(T.off[:, 0:64:2], T.pm[:], 512.0, None, A.add))
-    i_off = v(V.tensor_scalar(T.off[:, 1:64:2], T.pm[:], 512.0, None, A.add))
-    SC.wait_ge(S.gi, n_gi)
-    j = s(SC.activation(T.base1[:], T.base[:], F.Identity, bias=1.0))
-    SC.wait_ge(S.v, i_po)
-    s(SC.activation(T.pb[:, 256:512], T.po[:, 16:272], F.Identity, bias=T.base[:, 0:1], scale=0.5))
-    SC.wait_ge(S.s, j)
-    j_pb = s(SC.activation(T.pb[:, 0:256], T.po[:, 15:271], F.Identity, bias=T.base1[:, 0:1], scale=0.5))
+        j = s(SC.activation(T.tile[:, 768 + t:1024:4], T.xp[:, 512 * t:512 * t + 528].indirect(T.lown[:, 0:4]), F.Copy))
 
     V.wait_ge(S.lists, n_near + n_away)
     for a in range(4):
-        i_l = v(V.tensor_scalar(T.lrecv[32 * a:32 * a + 32, :], T.reqs[32 * me:32 * me + 32, :], -1.0, 256.0, A.mult, A.add))
+        i_l = v(V.tensor_scalar(T.lrecv[32 * a:32 * a + 32, :], T.reqs[32 * me:32 * me + 32, :], -1.0, 272.0, A.mult, A.add))
     SC.wait_ge(S.v, i_l)
     V.wait_ge(S.v, i_l)
     for t in range(2):
@@ -307,25 +283,37 @@ def rank_program(g, core, T, topo):
         g.remote_dma_fused(tr, local_sem=S.local)
     g.wait_ge(S.local, 3 * (n_near + n_away))
 
-    V.wait_ge(S.s, j_pb)
+    SC.wait_ge(S.gi, k_all)
+    s(SC.activation(T.pb[:, 257:513], T.po[:, 16:272], F.Identity, bias=T.qb[:, 0:1], scale=0.5))
+    j_pb = s(SC.activation(T.pb[:, 1:257], T.po[:, 15:271], F.Identity, bias=T.qb[:, 1:2], scale=0.5))
+    V.wait_ge(S.w, 16)
+    i_w = v(V.quantize_mx(T.wq[:, 0:256], T.wsc[:, 0:256], T.wt[:]))
+    V.wait_ge(S.gi, k_all)
+    V.wait_ge(S.wl16, 128)
+    i = v(V.tensor_scalar(T.nn[:], T.wl16[:], T.qb[:, 2:3], 0.0, A.add, A.max))
+    V.wait_ge(S.v, i)
+    for h in range(2):
+        i_off = v(V.tensor_scalar(T.off[:, h:32:2], T.nn[:], 513.0, None, A.min))
     V.wait_ge(S.v, i_off)
-    i = v(V.tensor_copy(T.gs[:, 0:512], T.pb[:, 0:528].indirect(T.off[:, 0:32])))
+    V.wait_ge(S.s, j_pb)
+    i = v(V.tensor_copy(T.gs[:, 0:256], T.pb[:, 0:514].indirect(T.off[:, 0:16])))
     SC.wait_ge(S.v, i_off)
     SC.wait_ge(S.s, j_pb)
-    j = s(SC.activation(T.gs[:, 512:1024], T.pb[:, 0:528].indirect(T.off[:, 32:64]), F.Copy))
+    j = s(SC.activation(T.gs[:, 256:512], T.pb[:, 0:514].indirect(T.off[:, 16:32]), F.Copy))
     V.wait_ge(S.v, i)
     V.wait_ge(S.s, j)
     i = v(V.transpose(T.tg[:], T.gs[:]))
     V.wait_ge(S.v, i)
-    v(V.tensor_tensor(T.sa[0:32, :], T.tg[0:32, 0:1024:32], T.tg[32:64, 0:1024:32], A.add))
-    i = v(V.tensor_tensor(T.sb[0:32, :], T.tg[64:96, 0:1024:32], T.tg[96:128, 0:1024:32], A.add))
+    for h in range(2):
+        i = v(V.tensor_tensor(T.sa[0:64, 16 * h:16 * h + 16], T.tg[0:64, 16 * h:512:32], T.tg[64:128, 16 * h:512:32], A.add))
     V.wait_ge(S.v, i)
-    i = v(V.tensor_tensor(T.sc[0:32, :], T.sa[0:32, :], T.sb[0:32, :], A.add))
+    for a in range(2):
+        i = v(V.tensor_tensor(T.sc[32 * a:32 * a + 32, :], T.sa[0:32, :], T.sa[32:64, :], A.add))
     V.wait_ge(S.v, i)
-    for a in range(4):
-        v(V.tensor_copy(T.slot[32 * a:32 * a + 32, :], T.sc[0:32, :]))
+    for a in range(2):
+        v(V.tensor_copy(T.slot[64 * a:64 * a + 64, :], T.sc[0:64, :]))
 
-    g.tensor.wait_ge(S.v, i_q)
+    g.tensor.wait_ge(S.v, i_w)
     pe = {}
     for h in range(2):
         if h == 0:
@@ -347,6 +335,7 @@ def rank_program(g, core, T, topo):
     for e in range(4):
         o, k = e // 2, 16 * (e % 2)
         c = 256 * e
+        n = 10 if e in (1, 2) else 8
         r = slice(256 * o, 256 * o + 256)
         if e == 0:
             V.wait_ge(S.v, i)
@@ -354,8 +343,8 @@ def rank_program(g, core, T, topo):
         if e == 2:
             V.wait_ge(S.s, j)
             SC.wait_ge(S.s, j)
-        a = v(V.tensor_copy(T.yt[:, c:c + 128], T.res[:, r].indirect(T.slot[:, k:k + 8])))
-        b = s(SC.activation(T.yt[:, c + 128:c + 256], T.res[:, r].indirect(T.slot[:, k + 8:k + 16]), F.Copy))
+        a = v(V.tensor_copy(T.yt[:, c:c + 16 * n], T.res[:, r].indirect(T.slot[:, k:k + n])))
+        b = s(SC.activation(T.yt[:, c + 16 * n:c + 256], T.res[:, r].indirect(T.slot[:, k + n:k + 16]), F.Copy))
         if e == 0:
             SC.wait_ge(S.pe, pe[(1, 1)])
             j = s(SC.activation(T.res[:, 384:512], T.prod[:, 1536:1664], F.Copy))

@@ -22,7 +22,10 @@ SCRATCH = {
     "ini": ("sbuf", [128, 2], "float32"),
     "pat": ("sbuf", [128, 64], "bfloat16"),
     "qb": ("sbuf", [128, 4], "float32"),
-    "ones": ("sbuf", [128, 64], "bfloat16"),
+    "zeros": ("sbuf", [128, 256], "bfloat16"),
+    "spread": ("sbuf", [128, 8], "uint16"),
+    "hit": ("sbuf", [128, 64], "bfloat16"),
+    "ground": ("sbuf", [128, 1], "float32"),
     "wf": ("sbuf", [128, 4], "float32"),
     "b1": ("sbuf", [128, 128], ROW),
     "row": ("sbuf", [128, 128], ROW),
@@ -32,15 +35,14 @@ SCRATCH = {
     "soff": ("sbuf", [128, 8], "uint16"),
     "win": ("sbuf", [128, 4096], "bfloat16"),
     "wint": ("sbuf", [128, 1024], "bfloat16"),
-    "e2": ("sbuf", [128, 32], "bfloat16"),
-    "cn": ("sbuf", [128, 16], "float32"),
+    "cn": ("sbuf", [128, 64], "float32"),
     "b2": ("sbuf", [128, 512], "bfloat16"),
     "row2": ("sbuf", [128, 544], "bfloat16"),
     "pp": ("sbuf", [128, 256], "bfloat16"),
     "po": ("sbuf", [128, 272], "bfloat16"),
     "junk": ("sbuf", [128, 512], "bfloat16"),
     "mk": ("sbuf", [128, 512], "bfloat16"),
-    "req": ("sbuf", [128, 260], "float32"),
+    "req": ("sbuf", [128, 516], "float32"),
     "reqs": ("sbuf", [128, 12], "float32"),
     "lown": ("sbuf", [128, 4], "uint16"),
     "lrecv": ("sbuf", [128, 12], "uint16"),
@@ -126,7 +128,8 @@ def rank_program(g, core, T, topo):
         g.sync.dma_start(T.wl16[16 * a:16 * a + 16, :], T.want[:, h:h + 16]).then_inc(S.wl16, 16)
     g.sync.dma_start(T.wt[:], T.w[:]).then_inc(S.w, 16)
 
-    k_ramp = iota(T.ramp[:], [[1, 193]], -64)
+    k_ramp = iota(T.ramp[:, 64:193], [[1, 129]], 0)
+    k_bit = iota(T.ramp[:, 0:64], [[0, 4], [1, 2], [0, 8]], 0)
     k_dump = iota(T.dump[:], [[2, 4]], 2048, 8)
     k_ci = iota(T.ci[:], [[-32, 4]], 0)
     k_pat = iota(T.pat[:], [[0, 32], [-2, 2]], 2)
@@ -137,93 +140,101 @@ def rank_program(g, core, T, topo):
         at = 64 * (0 if q == me else 1 + mine.index(q)) - 1
         g.wait_ge(S.gi, cnt["gi"])
         k_all = iota(T.qb[32 * q:32 * q + 32, :], [[1 - 512 * q - at, 2], [1, 2]], at)
-    i_z = v(V.memset(T.win[:, 1024:1280], 0.0))
-    v(V.memset(T.ones[:], 1.0))
-    v(V.memset(T.half[0:64, :], 1024.0))
-    v(V.memset(T.half[64:128, :], 0.0))
+    v(V.memset(T.zeros[:], 0.0))
+    for c in range(4):
+        i_so = v(V.memset(T.spread[:, 2 * c:2 * c + 2], c))
+    for a in range(2):
+        v(V.memset(T.half[64 * a:64 * a + 64, :], 1024.0 * (1 - a)))
+        v(V.memset(T.ground[64 * a + 32:64 * a + 64, :], 0.0))
     V.wait_ge(S.gi, k_ramp)
     i_lane = v(V.transpose(T.lane[:], T.ramp[:, 64:96]))
+    V.wait_ge(S.gi, k_bit)
+    v(V.transpose(T.hit[:], T.ramp[:, 0:64]))
     V.wait_ge(S.v, i_lane)
+    for a in range(2):
+        i_g = v(V.tensor_scalar(T.ground[64 * a:64 * a + 32, :], T.lane[64 * a:64 * a + 32, 0:1], 16.0, None, A.is_ge))
     start, first = [0, 129, 226, 323], [0, 32, 32, 32]
     for c in range(4):
         n, a = 129 - first[c], 64 + first[c] - 32 * c
         v(V.tensor_scalar(T.d1[:, start[c]:start[c] + n], T.ramp[:, a:a + n], T.lane[:, 0:1], 4096.0, A.not_equal, A.mult))
-    SC.wait_ge(S.v, i_z)
-    for k in range(1, 4):
-        j_win = s(SC.activation(T.win[:, 1024 + 256 * k:1280 + 256 * k], T.win[:, 1024:1280], F.Copy))
     SC.wait_ge(S.v, i_lane)
     s(SC.activation(T.la[:], T.lane[:, 0:1], F.Sign, bias=-15.5))
     j = s(SC.activation(T.lb[:], T.lane[:, 0:1], F.Identity, bias=15.0, scale=-2.0))
+    SC.wait_ge(S.v, i_g)
+    for k in range(4):
+        j_win = s(SC.activation(T.win[:, 1024 + 256 * k:1280 + 256 * k], T.zeros[:], F.Identity, bias=T.ground[:, 0:1]))
     SC.wait_ge(S.s, j)
     j = s(SC.activation(T.lc[:], T.la[:], F.Identity, bias=T.lb[:, 0:1], scale=16.0))
     SC.wait_ge(S.s, j)
     SC.wait_ge(S.gi, k_pat)
     j = s(SC.activation(T.nb[:], T.ci[:], F.Identity, bias=T.lc[:, 0:1]))
     SC.wait_ge(S.s, j)
-    s(SC.activation(T.lo[:], T.nb[:, 0:2], F.Identity, bias=-1.0, scale=-1.0))
-    s(SC.activation(T.hi[:], T.nb[:, 0:2], F.Identity, bias=1.0, scale=-1.0))
-    j_con = s(SC.activation(T.ini[:], T.nb[:, 0:2], F.Identity, bias=16.0, scale=256.0))
+    s(SC.activation(T.lo[:], T.nb[:, 2:4], F.Identity, bias=-1.0, scale=-1.0))
+    s(SC.activation(T.hi[:], T.nb[:, 2:4], F.Identity, bias=1.0, scale=-1.0))
+    for c in range(2, 4):
+        s(SC.activation(T.ini[:, c - 2:c - 1], T.nb[:, c:c + 1], F.Identity, bias=-8.0 * c, scale=256.0 - 8 * c))
 
     V.wait_ge(S.wl, 16)
-    i = v(V.tensor_copy(T.wf[:], T.wl[:]))
-    V.wait_ge(S.v, i)
-    for c in range(4):
-        i = v(V.tensor_scalar(T.b1[:, 32 * c:32 * c + 32], T.win[:, 1024:1056], T.wf[:, c:c + 1], None, A.add))
-    v(V.tensor_copy(T.eq[:, 128:420:97], T.wf[:]))
+    i = v(V.tensor_copy(T.b1[:], T.wl[:, 0:4].indirect(T.spread[:, 0:8])))
+    v(V.tensor_copy(T.wf[:], T.wl[:]))
+    v(V.tensor_copy(T.eq[:, 128:420:97], T.wl[:]))
     V.wait_ge(S.v, i)
     i = v(V.transpose(T.row[:], T.b1[:]))
     V.wait_ge(S.v, i)
     V.wait_ge(S.gi, k_dump)
-    for c in range(4):
-        i = v(V.tensor_scalar(T.eq[:, start[c]:start[c] + 128 - first[c]], T.row[:, first[c]:128], T.wf[:, c:c + 1], T.dump[:, c:c + 1],
-                              A.is_equal, A.mult))
-    V.wait_ge(S.v, i)
-    i = v(V.tensor_tensor_scan(T.dist[:], T.eq[:], T.d1[:], 0.0, A.max, A.min))
+    m = [v(V.tensor_scalar(T.eq[:, start[c]:start[c] + 128 - first[c]], T.row[:, first[c]:128], T.wf[:, c:c + 1], T.dump[:, c:c + 1],
+                           A.is_equal, A.mult)) for c in range(4)]
+    for k, c in ((slice(0, 226), 1), (slice(226, 420), 3)):
+        V.wait_ge(S.v, m[c])
+        i = v(V.tensor_tensor_scan(T.dist[:, k], T.eq[:, k], T.d1[:, k], 0.0, A.max, A.min))
     V.wait_ge(S.v, i)
     ends = slice(128, 420, 97)
     i = v(V.tensor_scalar(T.soff[:, 0:4], T.dist[:, ends], T.half[:, 0:1], None, A.add))
     v(V.tensor_scalar(T.soff[0:64, 4:8], T.dist[64:128, ends], 1024.0, None, A.add))
+    v(V.tensor_scalar(T.soff[64:128, 4:8], T.dist[0:64, ends], 0.0, None, A.add))
     V.wait_ge(S.v, i)
     V.wait_ge(S.s, j_win)
-    v(V.tensor_copy(T.win[:, 0:4096].indirect(T.soff[:, 0:4]), T.ones[:]))
-    i = v(V.tensor_scalar(T.soff[64:128, 4:8], T.dist[0:64, ends], 0.0, None, A.add))
+    i = v(V.tensor_copy(T.win[:, 0:4096].indirect(T.soff[:, 0:4]), T.hit[:]))
     V.wait_ge(S.v, i)
-    i = v(V.tensor_copy(T.win[:, 0:4096].indirect(T.soff[:, 4:8]), T.ones[:]))
+    i = v(V.tensor_copy(T.win[:, 0:4096].indirect(T.soff[:, 4:8]), T.hit[:]))
 
     V.wait_ge(S.v, i)
-    i = v(V.transpose(T.wint[:], T.win[:, 1024:2048]))
-    V.wait_ge(S.v, i)
-    for q in range(4):
-        a, c = 64 * (q // 2), slice(512 * (q % 2), 512 * (q % 2) + 512, 16)
-        i = v(V.tensor_tensor(T.e2[32 * q:32 * q + 32, :], T.wint[a:a + 32, c], T.wint[a + 32:a + 64, c], A.max))
-    V.wait_ge(S.v, i)
-    i_cn = v(V.tensor_tensor(T.cn[:], T.e2[:, 0:32:2], T.e2[:, 1:32:2], A.max))
+    m = [v(V.transpose(T.wint[:, 512 * h:512 * h + 512], T.win[:, 1024 + 512 * h:1536 + 512 * h])) for h in range(2)]
+    for q in (0, 2, 1, 3):
+        a, c = 64 * (q // 2), slice(512 * (q % 2), 512 * (q % 2) + 512, 8)
+        V.wait_ge(S.v, m[q % 2])
+        i_cn = v(V.tensor_tensor_scan(T.cn[32 * q:32 * q + 32, :], T.wint[a:a + 32, c], T.wint[a + 32:a + 64, c], 0.0, A.subtract, A.max))
     SC.wait_ge(S.v, i_cn)
-    for b in range(4, 8):
-        j = s(SC.activation(T.b2[:, 64 * b:64 * b + 64], T.pat[:], F.Identity, bias=T.cn[:, 8 + b:9 + b], scale=T.cn[:, b:b + 1]))
     V.wait_ge(S.v, i_cn)
     V.wait_ge(S.gi, k_pad)
-    for b in range(4):
-        i = v(V.tensor_scalar(T.b2[:, 64 * b:64 * b + 64], T.pat[:], T.cn[:, b:b + 1], T.cn[:, 8 + b:9 + b], A.mult, A.add))
-    V.wait_ge(S.v, i)
+    made = []
     for h in range(2):
-        if h == 1:
-            V.wait_ge(S.s, j)
+        for b in range(4 * h, 4 * h + 4):
+            k, f1, f2 = slice(64 * b, 64 * b + 64), T.cn[:, 4 * b + 3:4 * b + 4], T.cn[:, 4 * b + 35:4 * b + 36]
+            if b % 4 < 2:
+                i = v(V.tensor_scalar(T.b2[:, k], T.pat[:], f1, f2, A.mult, A.add))
+            else:
+                j = s(SC.activation(T.b2[:, k], T.pat[:], F.Identity, bias=f2, scale=f1))
+        made.append((i, j))
+    for h in range(2):
+        V.wait_ge(S.v, made[h][0])
+        V.wait_ge(S.s, made[h][1])
         v(V.transpose(T.row2[:, 288 + 128 * h:416 + 128 * h], T.b2[:, 256 * h:256 * h + 256:2]))
         i = v(V.transpose(T.row2[:, 32 + 128 * h:160 + 128 * h], T.b2[:, 256 * h + 1:256 * h + 256:2]))
     V.wait_ge(S.v, i)
     i_p = v(V.tensor_tensor_scan(T.pp[:], T.row2[:, 288:544], T.row2[:, 31:287], 0.0, A.add, A.add))
+    i_po = v(V.tensor_tensor_scan(T.po[:, 16:272], T.row2[:, 288:544], T.row2[:, 32:288], 0.0, A.add, A.add))
 
     SC.wait_ge(S.v, i_p)
-    for c in range(2, 4):
-        j_cnt = s(SC.activation(T.junk[:, 256 * c - 512:256 * c - 272], T.pp[:, 16:256], F.Sign, bias=T.nb[:, c:c + 1],
-                                accum_out=T.req[:, 256 + c:257 + c]))
+    for c in range(2):
+        j_cnt = s(SC.activation(T.junk[:, 256 * c:256 * c + 256], T.pp[:], F.Sign, bias=T.nb[:, c:c + 1], accum_out=T.req[:, 512 + c:513 + c]))
     V.wait_ge(S.v, i_p)
-    m = [v(V.tensor_scalar(T.mk[:, 256 * c:256 * c + 256], T.pp[:], T.lo[:, c:c + 1], T.hi[:, c:c + 1], A.max, A.min)) for c in range(2)]
+    m = [v(V.tensor_scalar(T.mk[:, 256 * c:256 * c + 240 - 8 * c], T.pp[:, 16 + 8 * c:256], T.lo[:, c:c + 1], T.hi[:, c:c + 1], A.max, A.min))
+         for c in range(2)]
     for c in range(2):
         V.wait_ge(S.v, m[c])
-        k = 256 * c
-        i_req = v(V.tensor_tensor_scan(T.req[:, 2 + c:258:2], T.mk[:, k:k + 128], T.mk[:, k + 128:k + 256], T.ini[:, c:c + 1], A.add, A.add))
+        k, n = 256 * c, 120 - 4 * c
+        i_req = v(V.tensor_tensor_scan(T.req[:, 518 + c - 4 * n:515 + c:4], T.mk[:, k:k + n], T.mk[:, k + n:k + 2 * n], T.ini[:, c:c + 1], A.add, A.add))
 
     g.wait_ge(S.s, j_cnt)
     g.wait_ge(S.v, i_req)
@@ -231,7 +242,7 @@ def rank_program(g, core, T, topo):
     for q in mine:
         at = 4 * order(q).index(me)
         tr.append(RemoteDMATransfer(dst_ids=dst(q), dma_engine_mask=masks[q], remote_sem=S.lists,
-                                    src=T.req[:, 256:260], dst=T.reqs[:, at:at + 4]))
+                                    src=T.req[:, 512:516], dst=T.reqs[:, at:at + 4]))
     g.remote_dma_fused(tr, local_sem=S.local)
 
     V.wait_ge(S.x, 16)
@@ -243,11 +254,10 @@ def rank_program(g, core, T, topo):
         for o in range(2):
             j_xp = s(SC.activation(T.xp[:, 512 * t + o:512 * t + 512:2], T.xs[:, 1024 * o + t:1024 * o + 1024:4], F.Copy))
     v(V.memset(T.xp[:, 2048:2064], 0.0))
-    i_po = v(V.tensor_tensor_scan(T.po[:, 16:272], T.row2[:, 288:544], T.row2[:, 32:288], 0.0, A.add, A.add))
     V.wait_ge(S.v, i_req)
     V.wait_ge(S.s, j_cnt)
     for a in range(4):
-        i_own = v(V.tensor_scalar(T.lown[32 * a:32 * a + 32, :], T.req[32 * me:32 * me + 32, 256:260], -1.0, 272.0, A.mult, A.add))
+        i_own = v(V.tensor_scalar(T.lown[32 * a:32 * a + 32, :], T.req[32 * me:32 * me + 32, 512:516], -1.0, 256.0, A.mult, A.add))
     V.wait_ge(S.v, i_own)
     V.wait_ge(S.s, j_xp - 2)
     for t in range(2):
@@ -259,7 +269,7 @@ def rank_program(g, core, T, topo):
 
     V.wait_ge(S.lists, n_near + n_away)
     for a in range(4):
-        i_l = v(V.tensor_scalar(T.lrecv[32 * a:32 * a + 32, :], T.reqs[32 * me:32 * me + 32, :], -1.0, 272.0, A.mult, A.add))
+        i_l = v(V.tensor_scalar(T.lrecv[32 * a:32 * a + 32, :], T.reqs[32 * me:32 * me + 32, :], -1.0, 256.0, A.mult, A.add))
     SC.wait_ge(S.v, i_l)
     V.wait_ge(S.v, i_l)
     for t in range(2):

@@ -4,36 +4,30 @@ from concourse.mybir import dt, AluOpType, ActivationFunctionType
 A = AluOpType
 F = ActivationFunctionType
 ROW = "float16"
+BIG = 4096
 
 SCRATCH = {
     "wl": ("sbuf", [128, 4], "int32"),
     "wl16": ("sbuf", [128, 16], "int32"),
-    "ramp": ("sbuf", [128, 193], "bfloat16"),
+    "ramp": ("sbuf", [128, 68], "bfloat16"),
+    "bits": ("sbuf", [128, 128], "bfloat16"),
     "lane": ("sbuf", [128, 32], "bfloat16"),
     "dump": ("sbuf", [128, 4], "float32"),
-    "ci": ("sbuf", [128, 4], "float32"),
-    "la": ("sbuf", [128, 1], "float32"),
-    "lb": ("sbuf", [128, 1], "float32"),
-    "lc": ("sbuf", [128, 1], "float32"),
-    "d1": ("sbuf", [128, 420], "bfloat16"),
-    "nb": ("sbuf", [128, 4], "float32"),
+    "d1": ("sbuf", [128, 260], "bfloat16"),
+    "nb": ("sbuf", [128, 2], "float32"),
     "lo": ("sbuf", [128, 2], "float32"),
     "hi": ("sbuf", [128, 2], "float32"),
     "ini": ("sbuf", [128, 2], "float32"),
     "pat": ("sbuf", [128, 64], "bfloat16"),
     "qb": ("sbuf", [128, 4], "float32"),
     "zeros": ("sbuf", [128, 256], "bfloat16"),
-    "spread": ("sbuf", [128, 8], "uint16"),
     "hit": ("sbuf", [128, 64], "bfloat16"),
     "ground": ("sbuf", [128, 1], "float32"),
     "wf": ("sbuf", [128, 4], "float32"),
-    "b1": ("sbuf", [128, 128], ROW),
-    "row": ("sbuf", [128, 128], ROW),
-    "eq": ("sbuf", [128, 420], ROW),
-    "dist": ("sbuf", [128, 420], ROW),
-    "half": ("sbuf", [128, 1], "float32"),
-    "soff": ("sbuf", [128, 8], "uint16"),
-    "win": ("sbuf", [128, 4096], "bfloat16"),
+    "row": ("sbuf", [128, 64], "int32"),
+    "eq": ("sbuf", [128, 260], "float32"),
+    "soff": ("sbuf", [128, 264], "uint16"),
+    "win": ("sbuf", [128, 4608], "bfloat16"),
     "wint": ("sbuf", [128, 1024], "bfloat16"),
     "cn": ("sbuf", [128, 64], "float32"),
     "b2": ("sbuf", [128, 512], "bfloat16"),
@@ -62,11 +56,11 @@ SCRATCH = {
     "wsc": ("sbuf", [128, 256], "uint8"),
     "qx": ("sbuf", [128, 448], "float8_e4m3fn_x4"),
     "qs": ("sbuf", [128, 448], "uint8"),
-    "prod": ("psum", [128, 2048], "float32"),
+    "prod": ("psum", [128, 3072], "float32"),
     "res": ("sbuf", [128, 512], "float32"),
     "yt": ("sbuf", [128, 1024], "float32"),
 }
-SEMAPHORES = ["v", "s", "pe", "gi", "wl", "wl16", "x", "w", "y", "lists", "local", "arr_a", "arr_b"]
+SEMAPHORES = ["v", "s", "pe", "gi", "wl", "row", "wl16", "x", "w", "y", "lists", "local", "arr_a", "arr_b"]
 
 
 def rank_program(g, core, T, topo):
@@ -95,12 +89,18 @@ def rank_program(g, core, T, topo):
         if q not in share:
             share[q] = [e for e in topo.engines(core, cores[q]) if e not in far][::2]
     masks = {q: sum(1 << e for e in share[q]) for q in mine}
+    others = [e for e in topo.engines(core, cores[mine[0]]) if e not in far]
+    rest, n_rest = sum(1 << e for e in others), len(others)
     n_near = sum(len(share[q]) for q in mine if near(q))
     n_away = sum(len(share[q]) for q in away)
 
     def dst(q):
         rid, pid, _ = topo.addr(cores[q])
         return [DstId(rid=rid, pnc=pid)]
+
+    def quad(q):
+        a = 32 * (2 * (q % 2) + q // 2)
+        return slice(a, a + 32)
 
     cnt = {"v": 0, "s": 0, "gi": 0}
 
@@ -122,91 +122,87 @@ def rank_program(g, core, T, topo):
     V, SC = g.vector, g.scalar
 
     g.sync.dma_start(T.wl[:], T.want[:]).then_inc(S.wl, 16)
+    for a in range(16):
+        (g.sync if a % 2 else g.scalar).dma_start(T.row[a:128:16, :], T.want[:]).then_inc(S.row, 16)
     g.sync.dma_start(T.xs[:], T.x[:]).then_inc(S.x, 16)
     for a in range(8):
         h = 16 * (a % 2)
         g.sync.dma_start(T.wl16[16 * a:16 * a + 16, :], T.want[:, h:h + 16]).then_inc(S.wl16, 16)
     g.sync.dma_start(T.wt[:], T.w[:]).then_inc(S.w, 16)
 
-    k_ramp = iota(T.ramp[:, 64:193], [[1, 129]], 0)
-    k_bit = iota(T.ramp[:, 0:64], [[0, 4], [1, 2], [0, 8]], 0)
-    k_dump = iota(T.dump[:], [[2, 4]], 2048, 8)
-    k_ci = iota(T.ci[:], [[-32, 4]], 0)
+    k_lane = iota(T.bits[:, 0:32], [[0, 2], [4 * BIG, 16]], 0)
+    k_ramp = iota(T.ramp[:], [[BIG, 68]], -3 * BIG)
+    k_dump = iota(T.dump[:], [[1, 4]], 3072, 4)
+    k_bit = iota(T.bits[:, 32:96], [[0, 4], [1, 2], [0, 8]], 0)
     k_pat = iota(T.pat[:], [[0, 32], [-2, 2]], 2)
     k_pad = iota(T.row2[:, 30:32], [[0, 2]], 0)
     iota(T.po[:, 14:16], [[0, 2]], 0)
     iota(T.pb[:, 0:514:513], [[0, 2]], 0)
     for q in range(4):
-        at = 64 * (0 if q == me else 1 + mine.index(q)) - 1
+        at = 64 * ([me] + away + mine[:1]).index(q) - 1
         g.wait_ge(S.gi, cnt["gi"])
-        k_all = iota(T.qb[32 * q:32 * q + 32, :], [[1 - 512 * q - at, 2], [1, 2]], at)
+        k_all = iota(T.qb[quad(q), :], [[1 - 512 * q - at, 2], [1, 2]], at)
+    for a in range(2):
+        i = v(V.memset(T.ground[64 * a:64 * a + 64, :], 1.0 - a))
     v(V.memset(T.zeros[:], 0.0))
-    for c in range(4):
-        i_so = v(V.memset(T.spread[:, 2 * c:2 * c + 2], c))
+    V.wait_ge(S.gi, k_lane)
+    i_lane = v(V.transpose(T.lane[:], T.bits[:, 0:32]))
+    V.wait_ge(S.v, i)
     for a in range(2):
-        v(V.memset(T.half[64 * a:64 * a + 64, :], 1024.0 * (1 - a)))
-        v(V.memset(T.ground[64 * a + 32:64 * a + 64, :], 0.0))
-    V.wait_ge(S.gi, k_ramp)
-    i_lane = v(V.transpose(T.lane[:], T.ramp[:, 64:96]))
-    V.wait_ge(S.gi, k_bit)
-    v(V.transpose(T.hit[:], T.ramp[:, 0:64]))
-    V.wait_ge(S.v, i_lane)
-    for a in range(2):
-        i_g = v(V.tensor_scalar(T.ground[64 * a:64 * a + 32, :], T.lane[64 * a:64 * a + 32, 0:1], 16.0, None, A.is_ge))
-    start, first = [0, 129, 226, 323], [0, 32, 32, 32]
-    for c in range(4):
-        n, a = 129 - first[c], 64 + first[c] - 32 * c
-        v(V.tensor_scalar(T.d1[:, start[c]:start[c] + n], T.ramp[:, a:a + n], T.lane[:, 0:1], 4096.0, A.not_equal, A.mult))
+        i_g = v(V.memset(T.ground[32 * a:32 * a + 16, :], 0.0))
     SC.wait_ge(S.v, i_lane)
-    s(SC.activation(T.la[:], T.lane[:, 0:1], F.Sign, bias=-15.5))
-    j = s(SC.activation(T.lb[:], T.lane[:, 0:1], F.Identity, bias=15.0, scale=-2.0))
+    SC.wait_ge(S.gi, k_ramp)
+    for c in range(4):
+        j_d1 = s(SC.activation(T.d1[:, 65 * c:65 * c + 65], T.ramp[:, 3 - c:68 - c], F.Abs, bias=T.lane[:, 0:1], scale=-1.0))
     SC.wait_ge(S.v, i_g)
     for k in range(4):
         j_win = s(SC.activation(T.win[:, 1024 + 256 * k:1280 + 256 * k], T.zeros[:], F.Identity, bias=T.ground[:, 0:1]))
-    SC.wait_ge(S.s, j)
-    j = s(SC.activation(T.lc[:], T.la[:], F.Identity, bias=T.lb[:, 0:1], scale=16.0))
-    SC.wait_ge(S.s, j)
-    SC.wait_ge(S.gi, k_pat)
-    j = s(SC.activation(T.nb[:], T.ci[:], F.Identity, bias=T.lc[:, 0:1]))
-    SC.wait_ge(S.s, j)
-    s(SC.activation(T.lo[:], T.nb[:, 2:4], F.Identity, bias=-1.0, scale=-1.0))
-    s(SC.activation(T.hi[:], T.nb[:, 2:4], F.Identity, bias=1.0, scale=-1.0))
-    for c in range(2, 4):
-        s(SC.activation(T.ini[:, c - 2:c - 1], T.nb[:, c:c + 1], F.Identity, bias=-8.0 * c, scale=256.0 - 8 * c))
+    for c in range(2):
+        u, n = 0.5 / BIG, 240 - 8 * c
+        for out, k, b in ((T.nb, -u, -32 * c - 1), (T.lo, u, 32 * c + 64), (T.hi, u, 32 * c + 66), (T.ini, -n * u, -n * (32 * c + 65) - 256 + n)):
+            s(SC.activation(out[:, c:c + 1], T.lane[:, 0:1], F.Identity, bias=float(b), scale=k))
 
     V.wait_ge(S.wl, 16)
-    i = v(V.tensor_copy(T.b1[:], T.wl[:, 0:4].indirect(T.spread[:, 0:8])))
-    v(V.tensor_copy(T.wf[:], T.wl[:]))
-    v(V.tensor_copy(T.eq[:, 128:420:97], T.wl[:]))
+    i = v(V.tensor_copy(T.wf[:], T.wl[:]))
+    for a in range(4):
+        v(V.tensor_scalar(T.eq[32 * a:32 * a + 32, 64:260:65], T.wl[32 * a:32 * a + 32, :], 1024.0 * (1 - a % 2), None, A.add))
+    V.wait_ge(S.gi, k_bit)
+    v(V.transpose(T.hit[:], T.bits[:, 32:96]))
     V.wait_ge(S.v, i)
-    i = v(V.transpose(T.row[:], T.b1[:]))
-    V.wait_ge(S.v, i)
-    V.wait_ge(S.gi, k_dump)
-    m = [v(V.tensor_scalar(T.eq[:, start[c]:start[c] + 128 - first[c]], T.row[:, first[c]:128], T.wf[:, c:c + 1], T.dump[:, c:c + 1],
-                           A.is_equal, A.mult)) for c in range(4)]
-    for k, c in ((slice(0, 226), 1), (slice(226, 420), 3)):
+    V.wait_ge(S.row, 256)
+    m = [v(V.tensor_scalar(T.eq[:, 65 * c:65 * c + 64], T.row[:], T.wf[:, c:c + 1], T.dump[:, c:c + 1], A.is_equal, A.mult)) for c in range(4)]
+    V.wait_ge(S.s, j_d1)
+    for c in range(4):
         V.wait_ge(S.v, m[c])
-        i = v(V.tensor_tensor_scan(T.dist[:, k], T.eq[:, k], T.d1[:, k], 0.0, A.max, A.min))
-    V.wait_ge(S.v, i)
-    ends = slice(128, 420, 97)
-    i = v(V.tensor_scalar(T.soff[:, 0:4], T.dist[:, ends], T.half[:, 0:1], None, A.add))
-    v(V.tensor_scalar(T.soff[0:64, 4:8], T.dist[64:128, ends], 1024.0, None, A.add))
-    v(V.tensor_scalar(T.soff[64:128, 4:8], T.dist[0:64, ends], 0.0, None, A.add))
+        k = slice(65 * c, 65 * c + 65)
+        i = v(V.tensor_tensor_scan(T.soff[:, c:260:4], T.eq[:, k], T.d1[:, k], 0.0, A.max, A.min))
+    SC.wait_ge(S.v, i)
+    for a in range(4):
+        b = a ^ 1
+        j = s(SC.activation(T.soff[32 * a:32 * a + 32, 260:264], T.soff[32 * b:32 * b + 32, 256:260], F.Identity, bias=1024.0 * (b - a)))
     V.wait_ge(S.v, i)
     V.wait_ge(S.s, j_win)
-    i = v(V.tensor_copy(T.win[:, 0:4096].indirect(T.soff[:, 0:4]), T.hit[:]))
+    i = v(V.tensor_copy(T.win[:].indirect(T.soff[:, 256:260]), T.hit[:]))
     V.wait_ge(S.v, i)
-    i = v(V.tensor_copy(T.win[:, 0:4096].indirect(T.soff[:, 4:8]), T.hit[:]))
+    V.wait_ge(S.s, j)
+    i = v(V.tensor_copy(T.win[:].indirect(T.soff[:, 260:264]), T.hit[:]))
+    SC.wait_ge(S.gi, k_pat)
+    SC.wait_ge(S.x, 16)
+    for o in range(2):
+        s(SC.activation(T.xp[:, 1536 + o:2048:2], T.xs[:, 1024 * o + 3:1024 * o + 1024:4], F.Copy))
 
     V.wait_ge(S.v, i)
     m = [v(V.transpose(T.wint[:, 512 * h:512 * h + 512], T.win[:, 1024 + 512 * h:1536 + 512 * h])) for h in range(2)]
-    for q in (0, 2, 1, 3):
-        a, c = 64 * (q // 2), slice(512 * (q % 2), 512 * (q % 2) + 512, 8)
-        V.wait_ge(S.v, m[q % 2])
-        i_cn = v(V.tensor_tensor_scan(T.cn[32 * q:32 * q + 32, :], T.wint[a:a + 32, c], T.wint[a + 32:a + 64, c], 0.0, A.subtract, A.max))
+    for h in range(2):
+        c = slice(512 * h, 512 * h + 512, 8)
+        V.wait_ge(S.v, m[h])
+        i_cn = v(V.tensor_tensor_scan(T.cn[64 * h:64 * h + 64, :], T.wint[0:64, c], T.wint[64:128, c], 0.0, A.subtract, A.max))
+    V.wait_ge(S.gi, k_all)
+    V.wait_ge(S.wl16, 128)
+    v(V.tensor_scalar(T.nn[:], T.wl16[:], T.qb[:, 2:3], 0.0, A.add, A.max))
+    v(V.memset(T.xp[:, 2048:2064], 0.0))
     SC.wait_ge(S.v, i_cn)
     V.wait_ge(S.v, i_cn)
-    V.wait_ge(S.gi, k_pad)
     made = []
     for h in range(2):
         for b in range(4 * h, 4 * h + 4):
@@ -221,6 +217,8 @@ def rank_program(g, core, T, topo):
         V.wait_ge(S.s, made[h][1])
         v(V.transpose(T.row2[:, 288 + 128 * h:416 + 128 * h], T.b2[:, 256 * h:256 * h + 256:2]))
         i = v(V.transpose(T.row2[:, 32 + 128 * h:160 + 128 * h], T.b2[:, 256 * h + 1:256 * h + 256:2]))
+    for h in range(2):
+        v(V.tensor_scalar(T.off[:, h:32:2], T.nn[:], 513.0, None, A.min))
     V.wait_ge(S.v, i)
     i_p = v(V.tensor_tensor_scan(T.pp[:], T.row2[:, 288:544], T.row2[:, 31:287], 0.0, A.add, A.add))
     i_po = v(V.tensor_tensor_scan(T.po[:, 16:272], T.row2[:, 288:544], T.row2[:, 32:288], 0.0, A.add, A.add))
@@ -246,119 +244,110 @@ def rank_program(g, core, T, topo):
     g.remote_dma_fused(tr, local_sem=S.local)
 
     V.wait_ge(S.x, 16)
-    SC.wait_ge(S.x, 16)
-    for t in range(2):
+    for t in range(3):
         for o in range(2):
             v(V.tensor_copy(T.xp[:, 512 * t + o:512 * t + 512:2], T.xs[:, 1024 * o + t:1024 * o + 1024:4]))
-    for t in range(2, 4):
-        for o in range(2):
-            j_xp = s(SC.activation(T.xp[:, 512 * t + o:512 * t + 512:2], T.xs[:, 1024 * o + t:1024 * o + 1024:4], F.Copy))
-    v(V.memset(T.xp[:, 2048:2064], 0.0))
     V.wait_ge(S.v, i_req)
     V.wait_ge(S.s, j_cnt)
     for a in range(4):
-        i_own = v(V.tensor_scalar(T.lown[32 * a:32 * a + 32, :], T.req[32 * me:32 * me + 32, 512:516], -1.0, 256.0, A.mult, A.add))
+        i_own = v(V.tensor_scalar(T.lown[32 * a:32 * a + 32, :], T.req[quad(me), 512:516], -1.0, 256.0, A.mult, A.add))
+    V.wait_ge(S.w, 16)
+    i_w = v(V.quantize_mx(T.wq[:, 0:256], T.wsc[:, 0:256], T.wt[:]))
     V.wait_ge(S.v, i_own)
-    V.wait_ge(S.s, j_xp - 2)
     for t in range(2):
-        i = v(V.tensor_copy(T.tile[:, 768 + t:1024:4], T.xp[:, 512 * t:512 * t + 528].indirect(T.lown[:, 0:4])))
-    SC.wait_ge(S.s, j_xp)
+        v(V.tensor_copy(T.tile[:, 768 + t:1024:4], T.xp[:, 512 * t:512 * t + 528].indirect(T.lown[:, 0:4])))
+    SC.wait_ge(S.gi, k_all)
+    SC.wait_ge(S.v, i_po)
+    s(SC.activation(T.pb[:, 257:513], T.po[:, 16:272], F.Identity, bias=T.qb[:, 0:1], scale=0.5))
+    j_pb = s(SC.activation(T.pb[:, 1:257], T.po[:, 15:271], F.Identity, bias=T.qb[:, 1:2], scale=0.5))
+    SC.wait_ge(S.s, j_pb)
+    s(SC.activation(T.gs[:, 0:256], T.pb[:, 0:514].indirect(T.off[:, 0:16]), F.Copy))
     SC.wait_ge(S.v, i_own)
     for t in range(2, 4):
-        j = s(SC.activation(T.tile[:, 768 + t:1024:4], T.xp[:, 512 * t:512 * t + 528].indirect(T.lown[:, 0:4]), F.Copy))
+        s(SC.activation(T.tile[:, 768 + t:1024:4], T.xp[:, 512 * t:512 * t + 528].indirect(T.lown[:, 0:4]), F.Copy))
 
     V.wait_ge(S.lists, n_near + n_away)
-    for a in range(4):
-        i_l = v(V.tensor_scalar(T.lrecv[32 * a:32 * a + 32, :], T.reqs[32 * me:32 * me + 32, :], -1.0, 256.0, A.mult, A.add))
-    SC.wait_ge(S.v, i_l)
-    V.wait_ge(S.v, i_l)
-    for t in range(2):
-        i = v(V.tensor_copy(T.tile[:, t:768:4], T.xp[:, 512 * t:512 * t + 528].indirect(T.lrecv[:, 0:12])))
-    for t in range(2, 4):
-        j = s(SC.activation(T.tile[:, t:768:4], T.xp[:, 512 * t:512 * t + 528].indirect(T.lrecv[:, 0:12]), F.Copy))
-    V.wait_ge(S.v, i)
-    V.wait_ge(S.s, j)
-    i_q = v(V.quantize_mx(T.qx[:, 0:256], T.qs[:, 0:256], T.tile[:]))
+    SC.wait_ge(S.lists, n_near + n_away)
+    for a in range(2):
+        i_l = v(V.tensor_scalar(T.lrecv[32 * a:32 * a + 32, :], T.reqs[quad(me), :], -1.0, 256.0, A.mult, A.add))
+        j_l = s(SC.activation(T.lrecv[32 * a + 64:32 * a + 96, :], T.reqs[quad(me), :], F.Identity, bias=256.0, scale=-1.0))
+    for e in (V, SC):
+        e.wait_ge(S.v, i_l)
+        e.wait_ge(S.s, j_l)
 
-    g.wait_ge(S.v, i_q)
-    for codes in (True, False):
+    def pick(t, a, b, k, n):
+        out, src = T.tile[:, 4 * a + t:4 * b:4], T.xp[:, 512 * t:512 * t + 528].indirect(T.lrecv[:, k:n])
+        return v(V.tensor_copy(out, src)) if t < 2 else s(SC.activation(out, src, F.Copy))
+
+    def send(to, codes):
         tr = []
-        for k, q in enumerate(mine):
-            at = 256 + 64 * order(q).index(me)
+        for k, q in to:
+            at = 256 + 64 * ((order(q).index(me) - 1) % 3)
             if codes:
                 a, b = T.qx[:, 64 * k:64 * k + 64].bitcast(dt.uint8), T.qx[:, at:at + 64].bitcast(dt.uint8)
             else:
                 a, b = T.qs[:, 64 * k:64 * k + 64], T.qs[:, at:at + 64]
-            tr.append(RemoteDMATransfer(dst_ids=dst(q), dma_engine_mask=masks[q], remote_sem=S.arr_a if near(q) else S.arr_b, src=a, dst=b))
+            tr.append(RemoteDMATransfer(dst_ids=dst(q), dma_engine_mask=rest if near(q) else masks[q],
+                                        remote_sem=S.arr_a if near(q) else S.arr_b, src=a, dst=b))
         g.remote_dma_fused(tr, local_sem=S.local)
-    g.wait_ge(S.local, 3 * (n_near + n_away))
 
-    SC.wait_ge(S.gi, k_all)
-    s(SC.activation(T.pb[:, 257:513], T.po[:, 16:272], F.Identity, bias=T.qb[:, 0:1], scale=0.5))
-    j_pb = s(SC.activation(T.pb[:, 1:257], T.po[:, 15:271], F.Identity, bias=T.qb[:, 1:2], scale=0.5))
-    V.wait_ge(S.w, 16)
-    i_w = v(V.quantize_mx(T.wq[:, 0:256], T.wsc[:, 0:256], T.wt[:]))
-    V.wait_ge(S.gi, k_all)
-    V.wait_ge(S.wl16, 128)
-    i = v(V.tensor_scalar(T.nn[:], T.wl16[:], T.qb[:, 2:3], 0.0, A.add, A.max))
-    V.wait_ge(S.v, i)
-    for h in range(2):
-        i_off = v(V.tensor_scalar(T.off[:, h:32:2], T.nn[:], 513.0, None, A.min))
-    V.wait_ge(S.v, i_off)
-    V.wait_ge(S.s, j_pb)
-    i = v(V.tensor_copy(T.gs[:, 0:256], T.pb[:, 0:514].indirect(T.off[:, 0:16])))
-    SC.wait_ge(S.v, i_off)
-    SC.wait_ge(S.s, j_pb)
+    done = [pick(t, 0, 128, 4, 12) for t in range(4)]
+    then = [pick(t, 128, 192, 0, 4) for t in range(4)]
+    V.wait_ge(S.v, done[1])
+    V.wait_ge(S.s, done[3])
+    g.wait_ge(S.v, v(V.quantize_mx(T.qx[:, 0:128], T.qs[:, 0:128], T.tile[:, 0:512])))
+    for codes in (True, False):
+        send(list(enumerate(away)), codes)
+    V.wait_ge(S.v, then[1])
+    V.wait_ge(S.s, then[3])
+    i_q = v(V.quantize_mx(T.qx[:, 128:256], T.qs[:, 128:256], T.tile[:, 512:1024]))
+    g.wait_ge(S.v, i_q)
+    for codes in (True, False):
+        send([(2, mine[0])], codes)
+    g.wait_ge(S.local, n_near + 3 * n_away + 2 * n_rest)
+
     j = s(SC.activation(T.gs[:, 256:512], T.pb[:, 0:514].indirect(T.off[:, 16:32]), F.Copy))
-    V.wait_ge(S.v, i)
     V.wait_ge(S.s, j)
     i = v(V.transpose(T.tg[:], T.gs[:]))
     V.wait_ge(S.v, i)
     for h in range(2):
         i = v(V.tensor_tensor(T.sa[0:64, 16 * h:16 * h + 16], T.tg[0:64, 16 * h:512:32], T.tg[64:128, 16 * h:512:32], A.add))
     V.wait_ge(S.v, i)
-    for a in range(2):
-        i = v(V.tensor_tensor(T.sc[32 * a:32 * a + 32, :], T.sa[0:32, :], T.sa[32:64, :], A.add))
-    V.wait_ge(S.v, i)
-    for a in range(2):
-        v(V.tensor_copy(T.slot[64 * a:64 * a + 64, :], T.sc[0:64, :]))
+    for a in range(4):
+        v(V.tensor_tensor(T.slot[32 * a:32 * a + 32, :], T.sa[0:32, :], T.sa[32:64, :], A.add))
 
-    g.tensor.wait_ge(S.v, i_w)
     pe = {}
-    for h in range(2):
-        if h == 0:
-            g.tensor.wait_ge(S.arr_a, 2 * n_near)
-        else:
-            g.tensor.wait_ge(S.arr_b, 2 * n_away)
-        c = slice(192 + 128 * h, 320 + 128 * h)
+    parts = [(S.v, i_q, 128, 64, 0), (S.arr_b, 2 * n_away, 256, 0, 64), (S.arr_a, 2 * n_rest, 320, 64, 192)]
+    for h, (sem, n, c, skip, at) in enumerate(parts):
+        g.tensor.wait_ge(sem, n)
         for o in range(2):
-            k = 2 * o + h
-            g.tensor.matmul_mx(T.prod[:, 512 * k:512 * k + 128], T.wq[:, 128 * o:128 * o + 128], T.wsc[:, 128 * o:128 * o + 128],
-                               T.qx[:, c], T.qs[:, c], True, True).then_inc(S.pe, 1)
-            pe[(o, h)] = len(pe) + 1
-    SC.wait_ge(S.pe, pe[(1, 0)])
-    s(SC.activation(T.res[:, 256:384], T.prod[:, 1024:1152], F.Copy))
-    for h in range(2):
-        V.wait_ge(S.pe, pe[(0, h)])
-        i = v(V.tensor_copy(T.res[:, 128 * h:128 * h + 128], T.prod[:, 512 * h:512 * h + 128]))
+            k = 512 * (2 * h + o)
+            g.tensor.matmul_mx(T.prod[:, k:k + 128], T.wq[:, 128 * o:128 * o + 128], T.wsc[:, 128 * o:128 * o + 128],
+                               T.qx[:, c:c + 128], T.qs[:, c:c + 128], True, True).then_inc(S.pe, 1)
+            pe[(o, h)] = (len(pe) + 1, T.res[:, 256 * o + at:256 * o + at + 128 - skip], T.prod[:, k + skip:k + 128])
+    for h in range(3):
+        V.wait_ge(S.pe, pe[(0, h)][0])
+        i = v(V.tensor_copy(*pe[(0, h)][1:]))
+        if h < 2:
+            SC.wait_ge(S.pe, pe[(1, h)][0])
+            s(SC.activation(*pe[(1, h)][1:], F.Copy))
 
-    for e in range(4):
-        o, k = e // 2, 16 * (e % 2)
-        c = 256 * e
-        n = 10 if e in (1, 2) else 8
+    stores = [(0, 0, 6, 12), (0, 12, 24, 32), (1, 0, 8, 16), (1, 16, 24, 32)]
+    for e, (o, k, n, end) in enumerate(stores):
+        c = 512 * o
         r = slice(256 * o, 256 * o + 256)
         if e == 0:
             V.wait_ge(S.v, i)
             SC.wait_ge(S.v, i)
-        if e == 2:
+        if (o, k) == (1, 0):
             V.wait_ge(S.s, j)
             SC.wait_ge(S.s, j)
-        a = v(V.tensor_copy(T.yt[:, c:c + 16 * n], T.res[:, r].indirect(T.slot[:, k:k + n])))
-        b = s(SC.activation(T.yt[:, c + 16 * n:c + 256], T.res[:, r].indirect(T.slot[:, k + n:k + 16]), F.Copy))
+        a = v(V.tensor_copy(T.yt[:, c + 16 * k:c + 16 * n], T.res[:, r].indirect(T.slot[:, k:n])))
+        b = s(SC.activation(T.yt[:, c + 16 * n:c + 16 * end], T.res[:, r].indirect(T.slot[:, n:end]), F.Copy))
         if e == 0:
-            SC.wait_ge(S.pe, pe[(1, 1)])
-            j = s(SC.activation(T.res[:, 384:512], T.prod[:, 1536:1664], F.Copy))
+            SC.wait_ge(S.pe, pe[(1, 2)][0])
+            j = s(SC.activation(*pe[(1, 2)][1:], F.Copy))
         g.sync.wait_ge(S.v, a)
         g.sync.wait_ge(S.s, b)
-        g.sync.dma_start(T.y[:, c:c + 256], T.yt[:, c:c + 256]).then_inc(S.y, 16)
-    g.sync.wait_ge(S.y, 64)
+        g.sync.dma_start(T.y[:, c + 16 * k:c + 16 * end], T.yt[:, c + 16 * k:c + 16 * end]).then_inc(S.y, 16)
+    g.sync.wait_ge(S.y, 16 * len(stores))

@@ -9,24 +9,25 @@ BIG = 4096
 SCRATCH = {
     "wl": ("sbuf", [128, 4], "int32"),
     "wl16": ("sbuf", [128, 16], "int32"),
-    "ramp": ("sbuf", [128, 68], "bfloat16"),
-    "bits": ("sbuf", [128, 128], "bfloat16"),
-    "lane": ("sbuf", [128, 32], "bfloat16"),
+    "bits": ("sbuf", [128, 225], "bfloat16"),
+    "lane": ("sbuf", [128, 64], "bfloat16"),
     "dump": ("sbuf", [128, 4], "float32"),
-    "d1": ("sbuf", [128, 260], "bfloat16"),
+    "d1": ("sbuf", [128, 129], "bfloat16"),
+    "spread": ("sbuf", [128, 8], "uint16"),
+    "b1": ("sbuf", [128, 128], ROW),
     "nb": ("sbuf", [128, 2], "float32"),
     "lo": ("sbuf", [128, 2], "float32"),
     "hi": ("sbuf", [128, 2], "float32"),
     "ini": ("sbuf", [128, 2], "float32"),
     "pat": ("sbuf", [128, 64], "bfloat16"),
     "qb": ("sbuf", [128, 4], "float32"),
-    "zeros": ("sbuf", [128, 256], "bfloat16"),
+    "zeros": ("sbuf", [128, 128], "bfloat16"),
     "hit": ("sbuf", [128, 64], "bfloat16"),
     "ground": ("sbuf", [128, 1], "float32"),
     "wf": ("sbuf", [128, 4], "float32"),
-    "row": ("sbuf", [128, 64], "int32"),
-    "eq": ("sbuf", [128, 260], "float32"),
-    "soff": ("sbuf", [128, 264], "uint16"),
+    "row": ("sbuf", [128, 128], ROW),
+    "eq": ("sbuf", [128, 516], "uint16"),
+    "soff": ("sbuf", [128, 520], "uint16"),
     "win": ("sbuf", [128, 4608], "bfloat16"),
     "wint": ("sbuf", [128, 1024], "bfloat16"),
     "cn": ("sbuf", [128, 64], "float32"),
@@ -37,9 +38,11 @@ SCRATCH = {
     "junk": ("sbuf", [128, 512], "bfloat16"),
     "mk": ("sbuf", [128, 512], "bfloat16"),
     "req": ("sbuf", [128, 516], "float32"),
-    "reqs": ("sbuf", [128, 12], "float32"),
+    "reqs": ("sbuf", [128, 4], "float32"),
     "lown": ("sbuf", [128, 4], "uint16"),
-    "lrecv": ("sbuf", [128, 12], "uint16"),
+    "lout": ("sbuf", [128, 8], "uint16"),
+    "lnear": ("sbuf", [128, 4], "uint16"),
+    "lfar": ("sbuf", [128, 8], "uint16"),
     "nn": ("sbuf", [128, 16], "float32"),
     "off": ("sbuf", [128, 32], "uint16"),
     "pb": ("sbuf", [128, 514], "bfloat16"),
@@ -60,7 +63,7 @@ SCRATCH = {
     "res": ("sbuf", [128, 512], "float32"),
     "yt": ("sbuf", [128, 1024], "float32"),
 }
-SEMAPHORES = ["v", "s", "pe", "gi", "wl", "row", "wl16", "x", "w", "y", "lists", "local", "arr_a", "arr_b"]
+SEMAPHORES = ["v", "s", "pe", "gi", "wl", "wl16", "x0", "x1", "w", "y", "list_a", "list_b", "local", "arr_a", "arr_b"]
 
 
 def rank_program(g, core, T, topo):
@@ -121,19 +124,25 @@ def rank_program(g, core, T, topo):
 
     V, SC = g.vector, g.scalar
 
+    def plane(t, u, n=2):
+        for o in range(2):
+            a, b = 512 * t + 256 * u, 1024 * u + 512 * o
+            out, src = T.xp[:, a + o:a + 256:2], T.xs[:, b + t:b + 512:4]
+            k = v(V.tensor_copy(out, src)) if t < n else s(SC.activation(out, src, F.Copy))
+        return k
+
     g.sync.dma_start(T.wl[:], T.want[:]).then_inc(S.wl, 16)
-    for a in range(16):
-        (g.sync if a % 2 else g.scalar).dma_start(T.row[a:128:16, :], T.want[:]).then_inc(S.row, 16)
-    g.sync.dma_start(T.xs[:], T.x[:]).then_inc(S.x, 16)
+    for o, sem in enumerate((S.x0, S.x1)):
+        g.sync.dma_start(T.xs[:, 1024 * o:1024 * o + 1024], T.x[:, 1024 * o:1024 * o + 1024]).then_inc(sem, 16)
     for a in range(8):
         h = 16 * (a % 2)
         g.sync.dma_start(T.wl16[16 * a:16 * a + 16, :], T.want[:, h:h + 16]).then_inc(S.wl16, 16)
     g.sync.dma_start(T.wt[:], T.w[:]).then_inc(S.w, 16)
 
-    k_lane = iota(T.bits[:, 0:32], [[0, 2], [4 * BIG, 16]], 0)
-    k_ramp = iota(T.ramp[:], [[BIG, 68]], -3 * BIG)
-    k_dump = iota(T.dump[:], [[1, 4]], 3072, 4)
-    k_bit = iota(T.bits[:, 32:96], [[0, 4], [1, 2], [0, 8]], 0)
+    k_ramp = iota(T.bits[:, 96:225], [[BIG, 129]], 0)
+    iota(T.dump[:], [[1, 4]], 3072, 4)
+    k_bit = iota(T.bits[:, 0:64], [[0, 4], [1, 2], [0, 8]], 0)
+    k_lane = iota(T.bits[:, 64:96], [[0, 2], [4 * BIG, 16]], 0)
     k_pat = iota(T.pat[:], [[0, 32], [-2, 2]], 2)
     k_pad = iota(T.row2[:, 30:32], [[0, 2]], 0)
     iota(T.po[:, 14:16], [[0, 2]], 0)
@@ -142,81 +151,106 @@ def rank_program(g, core, T, topo):
         at = 64 * ([me] + away + mine[:1]).index(q) - 1
         g.wait_ge(S.gi, cnt["gi"])
         k_all = iota(T.qb[quad(q), :], [[1 - 512 * q - at, 2], [1, 2]], at)
-    for a in range(2):
-        i = v(V.memset(T.ground[64 * a:64 * a + 64, :], 1.0 - a))
+    i = v(V.memset(T.ground[0:64, :], 1.0))
     v(V.memset(T.zeros[:], 0.0))
-    V.wait_ge(S.gi, k_lane)
-    i_lane = v(V.transpose(T.lane[:], T.bits[:, 0:32]))
+    v(V.memset(T.ground[64:128, :], 0.0))
+    v(V.memset(T.spread[:, 0:2], 0))
     V.wait_ge(S.v, i)
     for a in range(2):
         i_g = v(V.memset(T.ground[32 * a:32 * a + 16, :], 0.0))
-    SC.wait_ge(S.v, i_lane)
-    SC.wait_ge(S.gi, k_ramp)
-    for c in range(4):
-        j_d1 = s(SC.activation(T.d1[:, 65 * c:65 * c + 65], T.ramp[:, 3 - c:68 - c], F.Abs, bias=T.lane[:, 0:1], scale=-1.0))
+    i_sp = v(V.memset(T.spread[:, 2:4], 1))
+    V.wait_ge(S.gi, k_ramp)
+    i_lane = v(V.transpose(T.lane[:, 32:64], T.bits[:, 96:128]))
+
+    def clear(a, b):
+        for k in range(a, b):
+            j = s(SC.activation(T.win[:, 1024 + 128 * k:1152 + 128 * k], T.zeros[:], F.Identity, bias=T.ground[:, 0:1]))
+        return j
+
     SC.wait_ge(S.v, i_g)
-    for k in range(4):
-        j_win = s(SC.activation(T.win[:, 1024 + 256 * k:1280 + 256 * k], T.zeros[:], F.Identity, bias=T.ground[:, 0:1]))
+    for c in range(2, 4):
+        j = s(SC.activation(T.spread[:, 2 * c:2 * c + 2], T.zeros[:, 0:2], F.Identity, bias=float(c)))
+    clear(0, 2)
+    V.wait_ge(S.v, i_sp)
+    SC.wait_ge(S.s, j)
+
+    V.wait_ge(S.wl, 16)
+    SC.wait_ge(S.wl, 16)
+    i = v(V.tensor_copy(T.b1[:, 0:64], T.wl[:].indirect(T.spread[:, 0:4])))
+    j = s(SC.activation(T.b1[:, 64:128], T.wl[:].indirect(T.spread[:, 4:8]), F.Copy))
+    for a in range(1, 4):
+        s(SC.activation(T.eq[32 * a:32 * a + 32, 128:516:129], T.wl[32 * a:32 * a + 32, :], F.Identity, bias=1024.0 * (1 - a % 2)))
+    SC.wait_ge(S.v, i_lane)
+    j_end = s(SC.activation(T.d1[:], T.bits[:, 96:225], F.Abs, bias=T.lane[:, 32:33], scale=-1.0))
+    j_win = clear(2, 7)
+    v(V.tensor_copy(T.wf[:], T.wl[:]))
+    v(V.tensor_scalar(T.eq[0:32, 128:516:129], T.wl[0:32, :], 1024.0, None, A.add))
+    V.wait_ge(S.v, i)
+    V.wait_ge(S.s, j)
+    i = v(V.transpose(T.row[:], T.b1[:]))
+    v(V.tensor_scalar(T.win[:, 1920:2048], T.zeros[:], T.ground[:, 0:1], None, A.add))
+    V.wait_ge(S.gi, k_bit)
+    v(V.transpose(T.hit[:], T.bits[:, 0:64]))
+    V.wait_ge(S.v, i)
+    m = [v(V.tensor_scalar(T.eq[:, 161 * c:129 * c + 128], T.row[:, 32 * c:128], T.wf[:, c:c + 1], T.dump[:, c:c + 1], A.is_equal, A.mult))
+         for c in range(4)]
+    V.wait_ge(S.s, j_end)
+    for c in range(4):
+        V.wait_ge(S.v, m[c])
+        i = v(V.tensor_tensor_scan(T.soff[:, 129 * c:516:4], T.eq[:, 161 * c:129 * c + 129], T.d1[:, 0:129 - 32 * c], 0.0, A.max, A.min))
+    V.wait_ge(S.gi, k_lane)
+    i_l16 = v(V.transpose(T.lane[:, 0:32], T.bits[:, 64:96]))
+    SC.wait_ge(S.v, i)
+    for a in range(4):
+        b = a ^ 1
+        j = s(SC.activation(T.soff[32 * a:32 * a + 32, 516:520], T.soff[32 * b:32 * b + 32, 512:516], F.Identity, bias=1024.0 * (b - a)))
+    V.wait_ge(S.v, i)
+    V.wait_ge(S.s, j_win)
+    i = v(V.tensor_copy(T.win[:].indirect(T.soff[:, 512:516]), T.hit[:]))
+    V.wait_ge(S.v, i)
+    V.wait_ge(S.s, j)
+    i = v(V.tensor_copy(T.win[:].indirect(T.soff[:, 516:520]), T.hit[:]))
+    SC.wait_ge(S.v, i_l16)
     for c in range(2):
         u, n = 0.5 / BIG, 240 - 8 * c
         for out, k, b in ((T.nb, -u, -32 * c - 1), (T.lo, u, 32 * c + 64), (T.hi, u, 32 * c + 66), (T.ini, -n * u, -n * (32 * c + 65) - 256 + n)):
             s(SC.activation(out[:, c:c + 1], T.lane[:, 0:1], F.Identity, bias=float(b), scale=k))
-
-    V.wait_ge(S.wl, 16)
-    i = v(V.tensor_copy(T.wf[:], T.wl[:]))
-    for a in range(4):
-        v(V.tensor_scalar(T.eq[32 * a:32 * a + 32, 64:260:65], T.wl[32 * a:32 * a + 32, :], 1024.0 * (1 - a % 2), None, A.add))
-    V.wait_ge(S.gi, k_bit)
-    v(V.transpose(T.hit[:], T.bits[:, 32:96]))
-    V.wait_ge(S.v, i)
-    V.wait_ge(S.row, 256)
-    m = [v(V.tensor_scalar(T.eq[:, 65 * c:65 * c + 64], T.row[:], T.wf[:, c:c + 1], T.dump[:, c:c + 1], A.is_equal, A.mult)) for c in range(4)]
-    V.wait_ge(S.s, j_d1)
-    for c in range(4):
-        V.wait_ge(S.v, m[c])
-        k = slice(65 * c, 65 * c + 65)
-        i = v(V.tensor_tensor_scan(T.soff[:, c:260:4], T.eq[:, k], T.d1[:, k], 0.0, A.max, A.min))
-    SC.wait_ge(S.v, i)
-    for a in range(4):
-        b = a ^ 1
-        j = s(SC.activation(T.soff[32 * a:32 * a + 32, 260:264], T.soff[32 * b:32 * b + 32, 256:260], F.Identity, bias=1024.0 * (b - a)))
-    V.wait_ge(S.v, i)
-    V.wait_ge(S.s, j_win)
-    i = v(V.tensor_copy(T.win[:].indirect(T.soff[:, 256:260]), T.hit[:]))
-    V.wait_ge(S.v, i)
-    V.wait_ge(S.s, j)
-    i = v(V.tensor_copy(T.win[:].indirect(T.soff[:, 260:264]), T.hit[:]))
     SC.wait_ge(S.gi, k_pat)
-    SC.wait_ge(S.x, 16)
-    for o in range(2):
-        s(SC.activation(T.xp[:, 1536 + o:2048:2], T.xs[:, 1024 * o + 3:1024 * o + 1024:4], F.Copy))
+    SC.wait_ge(S.x0, 16)
+    V.wait_ge(S.gi, k_pat)
+    V.wait_ge(S.x0, 16)
+    for t in (3, 2, 0):
+        plane(t, 0)
 
     V.wait_ge(S.v, i)
-    m = [v(V.transpose(T.wint[:, 512 * h:512 * h + 512], T.win[:, 1024 + 512 * h:1536 + 512 * h])) for h in range(2)]
-    for h in range(2):
-        c = slice(512 * h, 512 * h + 512, 8)
-        V.wait_ge(S.v, m[h])
-        i_cn = v(V.tensor_tensor_scan(T.cn[64 * h:64 * h + 64, :], T.wint[0:64, c], T.wint[64:128, c], 0.0, A.subtract, A.max))
-    V.wait_ge(S.gi, k_all)
-    V.wait_ge(S.wl16, 128)
-    v(V.tensor_scalar(T.nn[:], T.wl16[:], T.qb[:, 2:3], 0.0, A.add, A.max))
-    v(V.memset(T.xp[:, 2048:2064], 0.0))
-    SC.wait_ge(S.v, i_cn)
-    V.wait_ge(S.v, i_cn)
+    m = [[v(V.transpose(T.wint[:, k:k + 256], T.win[:, 1024 + k:1280 + k])) for k in (256 * u, 512 + 256 * u)][1] for u in range(2)]
+    for u in range(2):
+        V.wait_ge(S.v, m[u])
+        for h in range(2):
+            c = slice(512 * h + 256 * u, 512 * h + 256 * u + 256, 8)
+            m[u] = v(V.tensor_tensor_scan(T.cn[64 * h:64 * h + 64, 32 * u:32 * u + 32], T.wint[0:64, c], T.wint[64:128, c], 0.0, A.subtract, A.max))
     made = []
-    for h in range(2):
-        for b in range(4 * h, 4 * h + 4):
-            k, f1, f2 = slice(64 * b, 64 * b + 64), T.cn[:, 4 * b + 3:4 * b + 4], T.cn[:, 4 * b + 35:4 * b + 36]
-            if b % 4 < 2:
-                i = v(V.tensor_scalar(T.b2[:, k], T.pat[:], f1, f2, A.mult, A.add))
+    for u in range(2):
+        SC.wait_ge(S.v, m[u])
+        V.wait_ge(S.v, m[u])
+        for b in range(4):
+            k, a = slice(256 * u + 64 * b, 256 * u + 64 * b + 64), 32 * u + 4 * b + 3
+            if b < 2:
+                i = v(V.tensor_scalar(T.b2[:, k], T.pat[:], T.cn[:, a:a + 1], T.cn[:, a + 16:a + 17], A.mult, A.add))
             else:
-                j = s(SC.activation(T.b2[:, k], T.pat[:], F.Identity, bias=f2, scale=f1))
+                j = s(SC.activation(T.b2[:, k], T.pat[:], F.Identity, bias=T.cn[:, a + 16:a + 17], scale=T.cn[:, a:a + 1]))
         made.append((i, j))
-    for h in range(2):
-        V.wait_ge(S.v, made[h][0])
-        V.wait_ge(S.s, made[h][1])
-        v(V.transpose(T.row2[:, 288 + 128 * h:416 + 128 * h], T.b2[:, 256 * h:256 * h + 256:2]))
-        i = v(V.transpose(T.row2[:, 32 + 128 * h:160 + 128 * h], T.b2[:, 256 * h + 1:256 * h + 256:2]))
+        if u == 0:
+            V.wait_ge(S.gi, k_all)
+            V.wait_ge(S.wl16, 128)
+            v(V.tensor_scalar(T.nn[:], T.wl16[:], T.qb[:, 2:3], 0.0, A.add, A.max))
+    for u in range(2):
+        V.wait_ge(S.v, made[u][0])
+        V.wait_ge(S.s, made[u][1])
+        v(V.transpose(T.row2[:, 288 + 128 * u:416 + 128 * u], T.b2[:, 256 * u:256 * u + 256:2]))
+        i = v(V.transpose(T.row2[:, 32 + 128 * u:160 + 128 * u], T.b2[:, 256 * u + 1:256 * u + 256:2]))
+        if u == 0:
+            v(V.memset(T.xp[:, 2048:2064], 0.0))
     for h in range(2):
         v(V.tensor_scalar(T.off[:, h:32:2], T.nn[:], 513.0, None, A.min))
     V.wait_ge(S.v, i)
@@ -236,48 +270,50 @@ def rank_program(g, core, T, topo):
 
     g.wait_ge(S.s, j_cnt)
     g.wait_ge(S.v, i_req)
-    tr = []
-    for q in mine:
-        at = 4 * order(q).index(me)
-        tr.append(RemoteDMATransfer(dst_ids=dst(q), dma_engine_mask=masks[q], remote_sem=S.lists,
-                                    src=T.req[:, 512:516], dst=T.reqs[:, at:at + 4]))
-    g.remote_dma_fused(tr, local_sem=S.local)
+    g.remote_dma_fused([RemoteDMATransfer(dst_ids=dst(mine[0]), dma_engine_mask=masks[mine[0]], remote_sem=S.list_a, src=T.req[:, 512:516], dst=T.reqs[:])],
+                       local_sem=S.local)
 
-    V.wait_ge(S.x, 16)
-    for t in range(3):
-        for o in range(2):
-            v(V.tensor_copy(T.xp[:, 512 * t + o:512 * t + 512:2], T.xs[:, 1024 * o + t:1024 * o + 1024:4]))
-    V.wait_ge(S.v, i_req)
-    V.wait_ge(S.s, j_cnt)
-    for a in range(4):
-        i_own = v(V.tensor_scalar(T.lown[32 * a:32 * a + 32, :], T.req[quad(me), 512:516], -1.0, 256.0, A.mult, A.add))
-    V.wait_ge(S.w, 16)
-    i_w = v(V.quantize_mx(T.wq[:, 0:256], T.wsc[:, 0:256], T.wt[:]))
-    V.wait_ge(S.v, i_own)
-    for t in range(2):
-        v(V.tensor_copy(T.tile[:, 768 + t:1024:4], T.xp[:, 512 * t:512 * t + 528].indirect(T.lown[:, 0:4])))
-    SC.wait_ge(S.gi, k_all)
-    SC.wait_ge(S.v, i_po)
-    s(SC.activation(T.pb[:, 257:513], T.po[:, 16:272], F.Identity, bias=T.qb[:, 0:1], scale=0.5))
-    j_pb = s(SC.activation(T.pb[:, 1:257], T.po[:, 15:271], F.Identity, bias=T.qb[:, 1:2], scale=0.5))
-    SC.wait_ge(S.s, j_pb)
-    s(SC.activation(T.gs[:, 0:256], T.pb[:, 0:514].indirect(T.off[:, 0:16]), F.Copy))
-    SC.wait_ge(S.v, i_own)
-    for t in range(2, 4):
-        s(SC.activation(T.tile[:, 768 + t:1024:4], T.xp[:, 512 * t:512 * t + 528].indirect(T.lown[:, 0:4]), F.Copy))
+    def lay(out, src, k=0):
+        for a in range(2):
+            i = v(V.tensor_scalar(out[32 * a:32 * a + 32, k:k + 4], src, -1.0, 256.0, A.mult, A.add))
+            j = s(SC.activation(out[32 * a + 64:32 * a + 96, k:k + 4], src, F.Identity, bias=256.0, scale=-1.0))
+        return i, j
 
-    V.wait_ge(S.lists, n_near + n_away)
-    SC.wait_ge(S.lists, n_near + n_away)
-    for a in range(2):
-        i_l = v(V.tensor_scalar(T.lrecv[32 * a:32 * a + 32, :], T.reqs[quad(me), :], -1.0, 256.0, A.mult, A.add))
-        j_l = s(SC.activation(T.lrecv[32 * a + 64:32 * a + 96, :], T.reqs[quad(me), :], F.Identity, bias=256.0, scale=-1.0))
+    def laid(e, ij):
+        e.wait_ge(S.v, ij[0])
+        e.wait_ge(S.s, ij[1])
+
+    for k in range(4):
+        a, o = 15 + 128 * (k // 2) + k % 2, k % 2
+        i_pb = v(V.tensor_scalar(T.pb[:, 1 + 128 * k:129 + 128 * k], T.po[:, a:a + 128], 0.5, T.qb[:, 1 - o:2 - o], A.mult, A.add))
+    SC.wait_ge(S.x1, 16)
+    plane(3, 1)
     for e in (V, SC):
-        e.wait_ge(S.v, i_l)
-        e.wait_ge(S.s, j_l)
+        laid(e, (i_req, j_cnt))
+    tr = []
+    for k, q in enumerate(away):
+        ij = lay(T.lout, T.req[quad(q), 512:516], 4 * k)
+        at = 4 * order(q).index(me) - 4
+        tr.append(RemoteDMATransfer(dst_ids=dst(q), dma_engine_mask=masks[q], remote_sem=S.list_b, src=T.lout[:, 4 * k:4 * k + 4], dst=T.lfar[:, at:at + 4]))
+    laid(g, ij)
+    g.remote_dma_fused(tr, local_sem=S.local)
+    own = lay(T.lown, T.req[quad(me), 512:516])
 
-    def pick(t, a, b, k, n):
-        out, src = T.tile[:, 4 * a + t:4 * b:4], T.xp[:, 512 * t:512 * t + 528].indirect(T.lrecv[:, k:n])
+    def pick(t, a, b, by):
+        out, src = T.tile[:, 4 * a + t:4 * b:4], T.xp[:, 512 * t:512 * t + 528].indirect(by)
         return v(V.tensor_copy(out, src)) if t < 2 else s(SC.activation(out, src, F.Copy))
+
+    V.wait_ge(S.x1, 16)
+    for t, o in ((2, 1), (1, 0), (1, 1), (0, 1)):
+        i_xp = plane(t, o, 3)
+    SC.wait_ge(S.v, i_pb)
+    s(SC.activation(T.gs[:, 0:256], T.pb[:, 0:514].indirect(T.off[:, 0:16]), F.Copy))
+    laid(SC, (i_xp - 6, own[1]))
+    laid(V, (i_xp - 2, own[1]))
+    for t in (3, 2, 1):
+        pick(t, 192, 256, T.lown[:])
+    V.wait_ge(S.v, i_xp)
+    pick(0, 192, 256, T.lown[:])
 
     def send(to, codes):
         tr = []
@@ -287,29 +323,35 @@ def rank_program(g, core, T, topo):
                 a, b = T.qx[:, 64 * k:64 * k + 64].bitcast(dt.uint8), T.qx[:, at:at + 64].bitcast(dt.uint8)
             else:
                 a, b = T.qs[:, 64 * k:64 * k + 64], T.qs[:, at:at + 64]
-            tr.append(RemoteDMATransfer(dst_ids=dst(q), dma_engine_mask=rest if near(q) else masks[q],
+            tr.append(RemoteDMATransfer(dst_ids=dst(q), dma_engine_mask=topo.mask(core, cores[q]) if near(q) else masks[q],
                                         remote_sem=S.arr_a if near(q) else S.arr_b, src=a, dst=b))
         g.remote_dma_fused(tr, local_sem=S.local)
 
-    done = [pick(t, 0, 128, 4, 12) for t in range(4)]
-    then = [pick(t, 128, 192, 0, 4) for t in range(4)]
-    V.wait_ge(S.v, done[1])
-    V.wait_ge(S.s, done[3])
+    for e in (V, SC):
+        e.wait_ge(S.list_a, n_near)
+    ij = lay(T.lnear, T.reqs[quad(me), :])
+    V.wait_ge(S.w, 16)
+    v(V.quantize_mx(T.wq[:, 0:128], T.wsc[:, 0:128], T.wt[:, 0:512]))
+    for e in (V, SC):
+        e.wait_ge(S.list_b, n_away)
+    done = [pick(t, 0, 128, T.lfar[:]) for t in range(4)]
+    for e in (V, SC):
+        laid(e, ij)
+    pick(0, 128, 192, T.lnear[:])
+    laid(V, done[1::2])
     g.wait_ge(S.v, v(V.quantize_mx(T.qx[:, 0:128], T.qs[:, 0:128], T.tile[:, 0:512])))
     for codes in (True, False):
         send(list(enumerate(away)), codes)
-    V.wait_ge(S.v, then[1])
-    V.wait_ge(S.s, then[3])
+    laid(V, [pick(t, 128, 192, T.lnear[:]) for t in range(1, 4)][0::2])
     i_q = v(V.quantize_mx(T.qx[:, 128:256], T.qs[:, 128:256], T.tile[:, 512:1024]))
     g.wait_ge(S.v, i_q)
     for codes in (True, False):
         send([(2, mine[0])], codes)
-    g.wait_ge(S.local, n_near + 3 * n_away + 2 * n_rest)
+    g.wait_ge(S.local, 5 * n_away + n_near + 2 * n_rest)
 
-    j = s(SC.activation(T.gs[:, 256:512], T.pb[:, 0:514].indirect(T.off[:, 16:32]), F.Copy))
-    V.wait_ge(S.s, j)
-    i = v(V.transpose(T.tg[:], T.gs[:]))
-    V.wait_ge(S.v, i)
+    i_w = v(V.quantize_mx(T.wq[:, 128:256], T.wsc[:, 128:256], T.wt[:, 512:1024]))
+    V.wait_ge(S.s, s(SC.activation(T.gs[:, 256:512], T.pb[:, 0:514].indirect(T.off[:, 16:32]), F.Copy)))
+    V.wait_ge(S.v, v(V.transpose(T.tg[:], T.gs[:])))
     for h in range(2):
         i = v(V.tensor_tensor(T.sa[0:64, 16 * h:16 * h + 16], T.tg[0:64, 16 * h:512:32], T.tg[64:128, 16 * h:512:32], A.add))
     V.wait_ge(S.v, i)
@@ -317,22 +359,22 @@ def rank_program(g, core, T, topo):
         v(V.tensor_tensor(T.slot[32 * a:32 * a + 32, :], T.sa[0:32, :], T.sa[32:64, :], A.add))
 
     pe = {}
-    parts = [(S.v, i_q, 128, 64, 0), (S.arr_b, 2 * n_away, 256, 0, 64), (S.arr_a, 2 * n_rest, 320, 64, 192)]
-    for h, (sem, n, c, skip, at) in enumerate(parts):
-        g.tensor.wait_ge(sem, n)
-        for o in range(2):
-            k = 512 * (2 * h + o)
-            g.tensor.matmul_mx(T.prod[:, k:k + 128], T.wq[:, 128 * o:128 * o + 128], T.wsc[:, 128 * o:128 * o + 128],
-                               T.qx[:, c:c + 128], T.qs[:, c:c + 128], True, True).then_inc(S.pe, 1)
-            pe[(o, h)] = (len(pe) + 1, T.res[:, 256 * o + at:256 * o + at + 128 - skip], T.prod[:, k + skip:k + 128])
+    parts = [(S.v, i_w, 128, 64, 0), (S.arr_b, 2 * n_away, 256, 0, 64), (S.arr_a, 2 * (n_rest + n_away), 320, 64, 192)]
+    for o, h in ((0, 0), (1, 0), (0, 1), (0, 2), (1, 1), (1, 2)):
+        sem, n, c, skip, at = parts[h]
+        if o == 0:
+            g.tensor.wait_ge(sem, n)
+        k = 512 * (2 * h + o)
+        g.tensor.matmul_mx(T.prod[:, k:k + 128], T.wq[:, 128 * o:128 * o + 128], T.wsc[:, 128 * o:128 * o + 128],
+                           T.qx[:, c:c + 128], T.qs[:, c:c + 128], True, True).then_inc(S.pe, 1)
+        pe[(o, h)] = (len(pe) + 1, T.res[:, 256 * o + at:256 * o + at + 128 - skip], T.prod[:, k + skip:k + 128])
     for h in range(3):
         V.wait_ge(S.pe, pe[(0, h)][0])
         i = v(V.tensor_copy(*pe[(0, h)][1:]))
-        if h < 2:
-            SC.wait_ge(S.pe, pe[(1, h)][0])
-            s(SC.activation(*pe[(1, h)][1:], F.Copy))
+        SC.wait_ge(S.pe, pe[(1, h)][0])
+        j = s(SC.activation(*pe[(1, h)][1:], F.Copy))
 
-    stores = [(0, 0, 6, 12), (0, 12, 24, 32), (1, 0, 8, 16), (1, 16, 24, 32)]
+    stores = [(0, 0, 8, 14), (0, 14, 24, 32), (1, 0, 8, 16), (1, 16, 24, 32)]
     for e, (o, k, n, end) in enumerate(stores):
         c = 512 * o
         r = slice(256 * o, 256 * o + 256)
@@ -344,9 +386,6 @@ def rank_program(g, core, T, topo):
             SC.wait_ge(S.s, j)
         a = v(V.tensor_copy(T.yt[:, c + 16 * k:c + 16 * n], T.res[:, r].indirect(T.slot[:, k:n])))
         b = s(SC.activation(T.yt[:, c + 16 * n:c + 16 * end], T.res[:, r].indirect(T.slot[:, n:end]), F.Copy))
-        if e == 0:
-            SC.wait_ge(S.pe, pe[(1, 2)][0])
-            j = s(SC.activation(*pe[(1, 2)][1:], F.Copy))
         g.sync.wait_ge(S.v, a)
         g.sync.wait_ge(S.s, b)
         g.sync.dma_start(T.y[:, c + 16 * k:c + 16 * end], T.yt[:, c + 16 * k:c + 16 * end]).then_inc(S.y, 16)

from concourse.bass import DstId, RemoteDMATransfer
from concourse.mybir import dt, AluOpType, ActivationFunctionType

A = AluOpType
F = ActivationFunctionType
ROW = "float16"
BIG = 4096

SCRATCH = {
    "wl": ("sbuf", [128, 4], "int32"),
    "wl16": ("sbuf", [128, 16], "int32"),
    "bits": ("sbuf", [128, 225], "bfloat16"),
    "lane": ("sbuf", [128, 64], "bfloat16"),
    "dump": ("sbuf", [128, 4], "float32"),
    "d1": ("sbuf", [128, 129], "bfloat16"),
    "spread": ("sbuf", [128, 8], "uint16"),
    "b1": ("sbuf", [128, 128], ROW),
    "nb": ("sbuf", [128, 2], "float32"),
    "lo": ("sbuf", [128, 2], "float32"),
    "hi": ("sbuf", [128, 2], "float32"),
    "ini": ("sbuf", [128, 2], "float32"),
    "pat": ("sbuf", [128, 64], "bfloat16"),
    "qb": ("sbuf", [128, 4], "float32"),
    "zeros": ("sbuf", [128, 128], "bfloat16"),
    "hit": ("sbuf", [128, 64], "bfloat16"),
    "ground": ("sbuf", [128, 1], "float32"),
    "wf": ("sbuf", [128, 4], "float32"),
    "row": ("sbuf", [128, 128], ROW),
    "eq": ("sbuf", [128, 516], "uint16"),
    "soff": ("sbuf", [128, 520], "uint16"),
    "win": ("sbuf", [128, 4608], "bfloat16"),
    "wint": ("sbuf", [128, 1024], "bfloat16"),
    "cn": ("sbuf", [128, 64], "float32"),
    "b2": ("sbuf", [128, 512], "bfloat16"),
    "row2": ("sbuf", [128, 544], "bfloat16"),
    "pp": ("sbuf", [128, 256], "bfloat16"),
    "po": ("sbuf", [128, 272], "bfloat16"),
    "junk": ("sbuf", [128, 512], "bfloat16"),
    "mk": ("sbuf", [128, 512], "bfloat16"),
    "req": ("sbuf", [128, 516], "float32"),
    "reqs": ("sbuf", [128, 4], "float32"),
    "lown": ("sbuf", [128, 4], "uint16"),
    "lout": ("sbuf", [128, 8], "uint16"),
    "lnear": ("sbuf", [128, 4], "uint16"),
    "lfar": ("sbuf", [128, 8], "uint16"),
    "nn": ("sbuf", [128, 16], "float32"),
    "off": ("sbuf", [128, 32], "uint16"),
    "pb": ("sbuf", [128, 514], "bfloat16"),
    "gs": ("sbuf", [128, 512], "bfloat16"),
    "tg": ("sbuf", [128, 512], "bfloat16"),
    "sa": ("sbuf", [128, 32], "float32"),
    "sc": ("sbuf", [128, 32], "float32"),
    "slot": ("sbuf", [128, 32], "uint16"),
    "xs": ("sbuf", [128, 2048], "bfloat16"),
    "xp": ("sbuf", [128, 2064], "bfloat16"),
    "tile": ("sbuf", [128, 1024], "bfloat16"),
    "wt": ("sbuf", [128, 1024], "bfloat16"),
    "wq": ("sbuf", [128, 256], "float8_e4m3fn_x4"),
    "wsc": ("sbuf", [128, 256], "uint8"),
    "qx": ("sbuf", [128, 448], "float8_e4m3fn_x4"),
    "qs": ("sbuf", [128, 448], "uint8"),
    "prod": ("psum", [128, 3072], "float32"),
    "res": ("sbuf", [128, 512], "float32"),
    "yt": ("sbuf", [128, 1024], "float32"),
}
SEMAPHORES = ["v", "s", "pe", "gi", "wl", "wl16", "x0", "x1", "w", "y", "list_a", "list_b", "local", "arr_a", "arr_b"]


def rank_program(g, core, T, topo):
    me = T.rank_of(core)
    if me is None:
        return
    cores = T.cores
    S = T.sem

    def near(q):
        return topo.chip(cores[q]) == topo.chip(core)

    def order(r):
        o = [q for q in range(len(cores)) if q != r]
        return sorted(o, key=lambda q: (topo.chip(cores[q]) != topo.chip(cores[r]), (q - r) % len(cores)))

    mine = order(me)
    away = [q for q in mine if not near(q)]
    share = {}
    far = []
    for k, q in enumerate(away):
        far = topo.engines(core, cores[q])
        w = len(far) // len(away)
        share[q] = far[k * w:(k + 1) * w]
    for q in mine:
        if q not in share:
            share[q] = [e for e in topo.engines(core, cores[q]) if e not in far][::2]
    masks = {q: sum(1 << e for e in share[q]) for q in mine}
    others = [e for e in topo.engines(core, cores[mine[0]]) if e not in far]
    rest, n_rest = sum(1 << e for e in others), len(others)
    n_near = sum(len(share[q]) for q in mine if near(q))
    n_away = sum(len(share[q]) for q in away)

    def dst(q):
        rid, pid, _ = topo.addr(cores[q])
        return [DstId(rid=rid, pnc=pid)]

    def quad(q):
        a = 32 * (2 * (q % 2) + q // 2)
        return slice(a, a + 32)

    cnt = {"v": 0, "s": 0, "gi": 0}

    def v(ins):
        cnt["v"] += 1
        ins.then_inc(S.v, 1)
        return cnt["v"]

    def s(ins):
        cnt["s"] += 1
        ins.then_inc(S.s, 1)
        return cnt["s"]

    def iota(out, pattern, base, step=0):
        cnt["gi"] += 1
        g.iota(out, pattern, base, step, allow_small_or_imprecise_dtypes=True).then_inc(S.gi, 1)
        return cnt["gi"]

    V, SC = g.vector, g.scalar

    def plane(t, u, n=2):
        for o in range(2):
            a, b = 512 * t + 256 * u, 1024 * u + 512 * o
            out, src = T.xp[:, a + o:a + 256:2], T.xs[:, b + t:b + 512:4]
            k = v(V.tensor_copy(out, src)) if t < n else s(SC.activation(out, src, F.Copy))
        return k

    g.sync.dma_start(T.wl[:], T.want[:]).then_inc(S.wl, 16)
    for o, sem in enumerate((S.x0, S.x1)):
        g.sync.dma_start(T.xs[:, 1024 * o:1024 * o + 1024], T.x[:, 1024 * o:1024 * o + 1024]).then_inc(sem, 16)
    for a in range(8):
        h = 16 * (a % 2)
        g.sync.dma_start(T.wl16[16 * a:16 * a + 16, :], T.want[:, h:h + 16]).then_inc(S.wl16, 16)
    g.sync.dma_start(T.wt[:], T.w[:]).then_inc(S.w, 16)

    k_ramp = iota(T.bits[:, 96:225], [[BIG, 129]], 0)
    iota(T.dump[:], [[1, 4]], 3072, 4)
    k_bit = iota(T.bits[:, 0:64], [[0, 4], [1, 2], [0, 8]], 0)
    k_lane = iota(T.bits[:, 64:96], [[0, 2], [4 * BIG, 16]], 0)
    k_pat = iota(T.pat[:], [[0, 32], [-2, 2]], 2)
    k_pad = iota(T.row2[:, 30:32], [[0, 2]], 0)
    iota(T.po[:, 14:16], [[0, 2]], 0)
    iota(T.pb[:, 0:514:513], [[0, 2]], 0)
    for q in range(4):
        at = 64 * ([me] + away + mine[:1]).index(q) - 1
        g.wait_ge(S.gi, cnt["gi"])
        k_all = iota(T.qb[quad(q), :], [[1 - 512 * q - at, 2], [1, 2]], at)
    i = v(V.memset(T.ground[0:64, :], 1.0))
    v(V.memset(T.zeros[:], 0.0))
    v(V.memset(T.ground[64:128, :], 0.0))
    v(V.memset(T.spread[:, 0:2], 0))
    V.wait_ge(S.v, i)
    for a in range(2):
        i_g = v(V.memset(T.ground[32 * a:32 * a + 16, :], 0.0))
    i_sp = v(V.memset(T.spread[:, 2:4], 1))
    V.wait_ge(S.gi, k_ramp)
    i_lane = v(V.transpose(T.lane[:, 32:64], T.bits[:, 96:128]))

    def clear(a, b):
        for k in range(a, b):
            j = s(SC.activation(T.win[:, 1024 + 128 * k:1152 + 128 * k], T.zeros[:], F.Identity, bias=T.ground[:, 0:1]))
        return j

    SC.wait_ge(S.v, i_g)
    for c in range(2, 4):
        j = s(SC.activation(T.spread[:, 2 * c:2 * c + 2], T.zeros[:, 0:2], F.Identity, bias=float(c)))
    clear(0, 2)
    V.wait_ge(S.v, i_sp)
    SC.wait_ge(S.s, j)

    V.wait_ge(S.wl, 16)
    SC.wait_ge(S.wl, 16)
    i = v(V.tensor_copy(T.b1[:, 0:64], T.wl[:].indirect(T.spread[:, 0:4])))
    j = s(SC.activation(T.b1[:, 64:128], T.wl[:].indirect(T.spread[:, 4:8]), F.Copy))
    for a in range(1, 4):
        s(SC.activation(T.eq[32 * a:32 * a + 32, 128:516:129], T.wl[32 * a:32 * a + 32, :], F.Identity, bias=1024.0 * (1 - a % 2)))
    SC.wait_ge(S.v, i_lane)
    j_end = s(SC.activation(T.d1[:], T.bits[:, 96:225], F.Abs, bias=T.lane[:, 32:33], scale=-1.0))
    j_win = clear(2, 7)
    v(V.tensor_copy(T.wf[:], T.wl[:]))
    v(V.tensor_scalar(T.eq[0:32, 128:516:129], T.wl[0:32, :], 1024.0, None, A.add))
    V.wait_ge(S.v, i)
    V.wait_ge(S.s, j)
    i = v(V.transpose(T.row[:], T.b1[:]))
    v(V.tensor_scalar(T.win[:, 1920:2048], T.zeros[:], T.ground[:, 0:1], None, A.add))
    V.wait_ge(S.gi, k_bit)
    v(V.transpose(T.hit[:], T.bits[:, 0:64]))
    V.wait_ge(S.v, i)
    m = [v(V.tensor_scalar(T.eq[:, 161 * c:129 * c + 128], T.row[:, 32 * c:128], T.wf[:, c:c + 1], T.dump[:, c:c + 1], A.is_equal, A.mult))
         for c in range(4)]
    V.wait_ge(S.s, j_end)
    for c in range(4):
        V.wait_ge(S.v, m[c])
        i = v(V.tensor_tensor_scan(T.soff[:, 129 * c:516:4], T.eq[:, 161 * c:129 * c + 129], T.d1[:, 0:129 - 32 * c], 0.0, A.max, A.min))
    V.wait_ge(S.gi, k_lane)
    i_l16 = v(V.transpose(T.lane[:, 0:32], T.bits[:, 64:96]))
    SC.wait_ge(S.v, i)
    for a in range(4):
        b = a ^ 1
        j = s(SC.activation(T.soff[32 * a:32 * a + 32, 516:520], T.soff[32 * b:32 * b + 32, 512:516], F.Identity, bias=1024.0 * (b - a)))
    V.wait_ge(S.v, i)
    V.wait_ge(S.s, j_win)
    i = v(V.tensor_copy(T.win[:].indirect(T.soff[:, 512:516]), T.hit[:]))
    V.wait_ge(S.v, i)
    V.wait_ge(S.s, j)
    i = v(V.tensor_copy(T.win[:].indirect(T.soff[:, 516:520]), T.hit[:]))
    SC.wait_ge(S.v, i_l16)
    for c in range(2):
        u, n = 0.5 / BIG, 240 - 8 * c
        for out, k, b in ((T.nb, -u, -32 * c - 1), (T.lo, u, 32 * c + 64), (T.hi, u, 32 * c + 66), (T.ini, -n * u, -n * (32 * c + 65) - 256 + n)):
            s(SC.activation(out[:, c:c + 1], T.lane[:, 0:1], F.Identity, bias=float(b), scale=k))
    SC.wait_ge(S.gi, k_pat)
    SC.wait_ge(S.x0, 16)
    V.wait_ge(S.gi, k_pat)
    V.wait_ge(S.x0, 16)
    for t in (3, 2, 0):
        plane(t, 0)

    V.wait_ge(S.v, i)
    m = [[v(V.transpose(T.wint[:, k:k + 256], T.win[:, 1024 + k:1280 + k])) for k in (256 * u, 512 + 256 * u)][1] for u in range(2)]
    for u in range(2):
        V.wait_ge(S.v, m[u])
        for h in range(2):
            c = slice(512 * h + 256 * u, 512 * h + 256 * u + 256, 8)
            m[u] = v(V.tensor_tensor_scan(T.cn[64 * h:64 * h + 64, 32 * u:32 * u + 32], T.wint[0:64, c], T.wint[64:128, c], 0.0, A.subtract, A.max))
    made = []
    for u in range(2):
        SC.wait_ge(S.v, m[u])
        V.wait_ge(S.v, m[u])
        for b in range(4):
            k, a = slice(256 * u + 64 * b, 256 * u + 64 * b + 64), 32 * u + 4 * b + 3
            if b < 2:
                i = v(V.tensor_scalar(T.b2[:, k], T.pat[:], T.cn[:, a:a + 1], T.cn[:, a + 16:a + 17], A.mult, A.add))
            else:
                j = s(SC.activation(T.b2[:, k], T.pat[:], F.Identity, bias=T.cn[:, a + 16:a + 17], scale=T.cn[:, a:a + 1]))
        made.append((i, j))
        if u == 0:
            V.wait_ge(S.gi, k_all)
            V.wait_ge(S.wl16, 128)
            v(V.tensor_scalar(T.nn[:], T.wl16[:], T.qb[:, 2:3], 0.0, A.add, A.max))
    for u in range(2):
        V.wait_ge(S.v, made[u][0])
        V.wait_ge(S.s, made[u][1])
        v(V.transpose(T.row2[:, 288 + 128 * u:416 + 128 * u], T.b2[:, 256 * u:256 * u + 256:2]))
        i = v(V.transpose(T.row2[:, 32 + 128 * u:160 + 128 * u], T.b2[:, 256 * u + 1:256 * u + 256:2]))
        if u == 0:
            v(V.memset(T.xp[:, 2048:2064], 0.0))
    for h in range(2):
        v(V.tensor_scalar(T.off[:, h:32:2], T.nn[:], 513.0, None, A.min))
    V.wait_ge(S.v, i)
    i_p = v(V.tensor_tensor_scan(T.pp[:], T.row2[:, 288:544], T.row2[:, 31:287], 0.0, A.add, A.add))
    i_po = v(V.tensor_tensor_scan(T.po[:, 16:272], T.row2[:, 288:544], T.row2[:, 32:288], 0.0, A.add, A.add))

    SC.wait_ge(S.v, i_p)
    for c in range(2):
        j_cnt = s(SC.activation(T.junk[:, 256 * c:256 * c + 256], T.pp[:], F.Sign, bias=T.nb[:, c:c + 1], accum_out=T.req[:, 512 + c:513 + c]))
    V.wait_ge(S.v, i_p)
    m = [v(V.tensor_scalar(T.mk[:, 256 * c:256 * c + 240 - 8 * c], T.pp[:, 16 + 8 * c:256], T.lo[:, c:c + 1], T.hi[:, c:c + 1], A.max, A.min))
         for c in range(2)]
    for c in range(2):
        V.wait_ge(S.v, m[c])
        k, n = 256 * c, 120 - 4 * c
        i_req = v(V.tensor_tensor_scan(T.req[:, 518 + c - 4 * n:515 + c:4], T.mk[:, k:k + n], T.mk[:, k + n:k + 2 * n], T.ini[:, c:c + 1], A.add, A.add))

    g.wait_ge(S.s, j_cnt)
    g.wait_ge(S.v, i_req)
    g.remote_dma_fused([RemoteDMATransfer(dst_ids=dst(mine[0]), dma_engine_mask=masks[mine[0]], remote_sem=S.list_a, src=T.req[:, 512:516], dst=T.reqs[:])],
                       local_sem=S.local)

    def lay(out, src, k=0):
        for a in range(2):
            i = v(V.tensor_scalar(out[32 * a:32 * a + 32, k:k + 4], src, -1.0, 256.0, A.mult, A.add))
            j = s(SC.activation(out[32 * a + 64:32 * a + 96, k:k + 4], src, F.Identity, bias=256.0, scale=-1.0))
        return i, j

    def laid(e, ij):
        e.wait_ge(S.v, ij[0])
        e.wait_ge(S.s, ij[1])

    for k in range(4):
        a, o = 15 + 128 * (k // 2) + k % 2, k % 2
        i_pb = v(V.tensor_scalar(T.pb[:, 1 + 128 * k:129 + 128 * k], T.po[:, a:a + 128], 0.5, T.qb[:, 1 - o:2 - o], A.mult, A.add))
    SC.wait_ge(S.x1, 16)
    plane(3, 1)
    for e in (V, SC):
        laid(e, (i_req, j_cnt))
    tr = []
    for k, q in enumerate(away):
        ij = lay(T.lout, T.req[quad(q), 512:516], 4 * k)
        at = 4 * order(q).index(me) - 4
        tr.append(RemoteDMATransfer(dst_ids=dst(q), dma_engine_mask=masks[q], remote_sem=S.list_b, src=T.lout[:, 4 * k:4 * k + 4], dst=T.lfar[:, at:at + 4]))
    laid(g, ij)
    g.remote_dma_fused(tr, local_sem=S.local)
    own = lay(T.lown, T.req[quad(me), 512:516])

    def pick(t, a, b, by):
        out, src = T.tile[:, 4 * a + t:4 * b:4], T.xp[:, 512 * t:512 * t + 528].indirect(by)
        return v(V.tensor_copy(out, src)) if t < 2 else s(SC.activation(out, src, F.Copy))

    V.wait_ge(S.x1, 16)
    for t, o in ((2, 1), (1, 0), (1, 1), (0, 1)):
        i_xp = plane(t, o, 3)
    SC.wait_ge(S.v, i_pb)
    s(SC.activation(T.gs[:, 0:256], T.pb[:, 0:514].indirect(T.off[:, 0:16]), F.Copy))
    laid(SC, (i_xp - 6, own[1]))
    laid(V, (i_xp - 2, own[1]))
    for t in (3, 2, 1):
        pick(t, 192, 256, T.lown[:])
    V.wait_ge(S.v, i_xp)
    pick(0, 192, 256, T.lown[:])

    def send(to, codes):
        tr = []
        for k, q in to:
            at = 256 + 64 * ((order(q).index(me) - 1) % 3)
            if codes:
                a, b = T.qx[:, 64 * k:64 * k + 64].bitcast(dt.uint8), T.qx[:, at:at + 64].bitcast(dt.uint8)
            else:
                a, b = T.qs[:, 64 * k:64 * k + 64], T.qs[:, at:at + 64]
            tr.append(RemoteDMATransfer(dst_ids=dst(q), dma_engine_mask=topo.mask(core, cores[q]) if near(q) else masks[q],
                                        remote_sem=S.arr_a if near(q) else S.arr_b, src=a, dst=b))
        g.remote_dma_fused(tr, local_sem=S.local)

    for e in (V, SC):
        e.wait_ge(S.list_a, n_near)
    ij = lay(T.lnear, T.reqs[quad(me), :])
    V.wait_ge(S.w, 16)
    v(V.quantize_mx(T.wq[:, 0:128], T.wsc[:, 0:128], T.wt[:, 0:512]))
    for e in (V, SC):
        e.wait_ge(S.list_b, n_away)
    done = [pick(t, 0, 128, T.lfar[:]) for t in range(4)]
    for e in (V, SC):
        laid(e, ij)
    pick(0, 128, 192, T.lnear[:])
    laid(V, done[1::2])
    g.wait_ge(S.v, v(V.quantize_mx(T.qx[:, 0:128], T.qs[:, 0:128], T.tile[:, 0:512])))
    for codes in (True, False):
        send(list(enumerate(away)), codes)
    laid(V, [pick(t, 128, 192, T.lnear[:]) for t in range(1, 4)][0::2])
    i_q = v(V.quantize_mx(T.qx[:, 128:256], T.qs[:, 128:256], T.tile[:, 512:1024]))
    g.wait_ge(S.v, i_q)
    for codes in (True, False):
        send([(2, mine[0])], codes)
    g.wait_ge(S.local, 5 * n_away + n_near + 2 * n_rest)

    i_w = v(V.quantize_mx(T.wq[:, 128:256], T.wsc[:, 128:256], T.wt[:, 512:1024]))
    V.wait_ge(S.s, s(SC.activation(T.gs[:, 256:512], T.pb[:, 0:514].indirect(T.off[:, 16:32]), F.Copy)))
    V.wait_ge(S.v, v(V.transpose(T.tg[:], T.gs[:])))
    for h in range(2):
        i = v(V.tensor_tensor(T.sa[0:64, 16 * h:16 * h + 16], T.tg[0:64, 16 * h:512:32], T.tg[64:128, 16 * h:512:32], A.add))
    V.wait_ge(S.v, i)
    for a in range(4):
        v(V.tensor_tensor(T.slot[32 * a:32 * a + 32, :], T.sa[0:32, :], T.sa[32:64, :], A.add))

    pe = {}
    parts = [(S.v, i_w, 128, 64, 0), (S.arr_b, 2 * n_away, 256, 0, 64), (S.arr_a, 2 * (n_rest + n_away), 320, 64, 192)]
    for o, h in ((0, 0), (1, 0), (0, 1), (0, 2), (1, 1), (1, 2)):
        sem, n, c, skip, at = parts[h]
        if o == 0:
            g.tensor.wait_ge(sem, n)
        k = 512 * (2 * h + o)
        g.tensor.matmul_mx(T.prod[:, k:k + 128], T.wq[:, 128 * o:128 * o + 128], T.wsc[:, 128 * o:128 * o + 128],
                           T.qx[:, c:c + 128], T.qs[:, c:c + 128], True, True).then_inc(S.pe, 1)
        pe[(o, h)] = (len(pe) + 1, T.res[:, 256 * o + at:256 * o + at + 128 - skip], T.prod[:, k + skip:k + 128])
    for h in range(3):
        V.wait_ge(S.pe, pe[(0, h)][0])
        i = v(V.tensor_copy(*pe[(0, h)][1:]))
        SC.wait_ge(S.pe, pe[(1, h)][0])
        j = s(SC.activation(*pe[(1, h)][1:], F.Copy))

    stores = [(0, 0, 8, 14), (0, 14, 24, 32), (1, 0, 8, 16), (1, 16, 24, 32)]
    for e, (o, k, n, end) in enumerate(stores):
        c = 512 * o
        r = slice(256 * o, 256 * o + 256)
        if e == 0:
            V.wait_ge(S.v, i)
            SC.wait_ge(S.v, i)
        if (o, k) == (1, 0):
            V.wait_ge(S.s, j)
            SC.wait_ge(S.s, j)
        a = v(V.tensor_copy(T.yt[:, c + 16 * k:c + 16 * n], T.res[:, r].indirect(T.slot[:, k:n])))
        b = s(SC.activation(T.yt[:, c + 16 * n:c + 16 * end], T.res[:, r].indirect(T.slot[:, n:end]), F.Copy))
        g.sync.wait_ge(S.v, a)
        g.sync.wait_ge(S.s, b)
        g.sync.dma_start(T.y[:, c + 16 * k:c + 16 * end], T.yt[:, c + 16 * k:c + 16 * end]).then_inc(S.y, 16)
    g.sync.wait_ge(S.y, 16 * len(stores))
